import numpy as np, ml_dtypes
CORES = [10,34,74,98]
N = 4
BF = ml_dtypes.bfloat16
W, Q, TV, HOP, M = 4096, 256, 8, 1, 9
def parts(rng):
    hi = rng.choice(np.array([64, 128, 192, 256]), (N, 8, 1, W)); p = np.floor(hi * rng.random((N, 8, 16, W)))
    lo = rng.choice(np.array([0, 32, 64, 128, 192]), (N, 8, 1, Q)); y = lo + np.floor((256 - lo) * rng.random((N, 8, 16, Q)))
    L = rng.integers(0, W, (N, 8, 16, Q)); share = rng.choice(np.array([0.0, 0.1, 0.3, 0.7, 1.0]), (N, 8, 1, Q))
    C = np.where(rng.random((N, 8, 16, Q)) < share, rng.integers(0, W, (N, 8, 16, Q)), -1)
    o = rng.integers(0, 16, (N, 8, 16, Q)); b = np.minimum(rng.integers(0, 8, (N, 8, 16, Q)), rng.integers(0, 8, (N, 8, 16, Q)))
    return p, y, L, C, o, b, rng.integers(0, 4, (N, 8, 16, TV))
def pack(p, y, L, C, o, b, lim):
    def half(a): return np.ascontiguousarray(np.asarray(a, np.float32).reshape(N, 128, -1)).astype(BF)
    def whole(a): return np.ascontiguousarray(np.asarray(a).reshape(N, 128, -1)).astype(np.int32)
    return {"prop": half(p), "lem": whole(L), "con": whole(C), "org": half(o), "cnt": half(b), "ex": half(y), "lim": whole(lim)}
def setup_inputs(rng):
    return pack(*parts(rng))
def setup_inputs_spread(rng):
    p, y, L, C, o, b, lim = parts(rng)
    p = np.minimum(np.floor(np.exp2(8 * rng.random((N, 8, 1, W))) * rng.random((N, 8, 16, W))), 255)
    y = np.minimum(np.floor(np.exp2(2 + 6 * rng.random((N, 8, 1, Q))) * rng.random((N, 8, 16, Q))), 255)
    y = np.where(rng.random((N, 8, 1, Q)) < 0.5, 255 - y, y)
    L = np.minimum(np.floor(W * rng.random((N, 8, 16, Q)) ** 3), W - 1)
    C = np.where(C >= 0, W - 1 - np.minimum(np.floor(W * rng.random((N, 8, 16, Q)) ** 3), W - 1), -1)
    o = np.minimum(np.floor(16 * rng.random((N, 8, 16, Q)) ** 2), 15); b = rng.integers(0, 8, (N, 8, 16, Q))
    return pack(p, y, L, C, o, b, lim)
def setup_inputs_ends(rng):
    p = 255 * (rng.random((N, 8, 16, W)) < rng.choice(np.array([0.0, 0.5, 1.0]), (N, 8, 1, W))).astype(np.int64)
    y = 255 * (rng.random((N, 8, 16, Q)) < rng.choice(np.array([0.0, 0.5, 1.0]), (N, 8, 1, Q))).astype(np.int64)
    just = np.argsort(rng.random((N, 8, 16, Q)), axis=2) < 16 - M
    y = np.where(rng.random((N, 8, 1, Q)) < 0.25, 255 * just, y)
    L = (W - 1) * rng.integers(0, 2, (N, 8, 16, Q)); share = rng.choice(np.array([0.0, 0.5, 1.0]), (N, 8, 1, Q))
    C = np.where(rng.random((N, 8, 16, Q)) < share, W - 1, -1)
    o = 15 * rng.integers(0, 2, (N, 8, 16, Q)); b = 7 * rng.integers(0, 2, (N, 8, 16, Q)); lim = 3 * rng.integers(0, 2, (N, 8, 16, TV))
    turn = int(rng.integers(0, 4))
    for r in range(N):
        for g in range(8):
            w = (r + g + turn) % 4
            if (r, g) in ((0, 0), (N - 1, 7)): w = 3
            if (r, g) in ((0, 7), (N - 1, 6)): w = 1
            pm = rng.permutation(16)
            p[r, g, :, 0] = (0 * pm, 0 * pm + 255, 255 * (pm < M), 0 * pm)[w]
            p[r, g, :, W - 1] = (0 * pm + 255, 0 * pm, 255 * (pm < M - 1), 0 * pm)[w]
            for c in (0, Q - 1):
                if w == 3: y[r, g, :, c] = 255
                if w == 1:
                    y[r, g, :, c] = 0; L[r, g, :, c] = W - 1; L[r, g, 15, c] = 0; C[r, g, :, c] = W - 1; C[r, g, 15, c] = -1
                if w == 0:
                    y[r, g, :, c] = 254 + (pm < 16 - M); L[r, g, :, c] = 0; L[r, g, 15, c] = W - 1; C[r, g, :, c] = 0
    return pack(p, y, L, C, o, b, lim)
def setup_inputs_corners(rng):
    p, y, L, C, o, b, lim = parts(rng)
    p[..., :W // 4] = np.floor(0.125 * p[..., :W // 4]); p[..., W // 2:] = 96 + np.floor(160 * rng.random((N, 8, 16, W - W // 2))); p[..., W - 1] = 255
    y = 32 + np.floor(224 * rng.random((N, 8, 16, Q))); y = np.where(rng.random((N, 8, 1, Q)) < 0.125, 255, y)
    e = (np.arange(Q).reshape(1, 1, 1, Q) + rng.integers(0, 6, (N, 8, 1, 1))) % 6; k = np.arange(16).reshape(1, 1, 16, 1)
    name = np.where(rng.random((N, 8, 1, Q)) < 0.6, rng.integers(0, W // 4, (N, 8, 16, Q)), rng.integers(0, W, (N, 8, 16, Q)))
    hole = rng.choice(np.array([0, 15, 15, 6]), (N, 8, 1, Q))
    has = np.where(e == 0, False, np.where(e == 2, k != hole, np.where(e == 3, k == 15, True)))
    C = np.where(has, name, -1)
    L = np.where(rng.random((N, 8, 1, Q)) < 0.5, rng.integers(W // 2, W, (N, 8, 16, Q)), L)
    mode = rng.integers(0, 4, (N, 8, 1, Q)); o = np.where(mode == 0, k, np.where(mode == 1, 0, np.where(mode == 2, 15, o)))
    b = rng.choice(np.array([0, 0, 1, 3, 6, 7]), (N, 8, 16, Q)); b = np.where(e == 4, 7, np.where(e == 5, 7 * (k == 15), b))
    lim = 3 * rng.integers(0, 2, (N, 8, 16, TV))
    for c in (Q - 2, Q - 1):
        y[:, :, :, c] = 0; C[:, :, :, c] = -1; C[:, :, 15, c] = W - 1; b[:, :, 15, c] = 0
    y[:, 0, :, Q - 2] = 255; C[:, 0, :, Q - 2] = -1
    return pack(p, y, L, C, o, b, lim)
def setup_inputs_ties(rng):
    p, y, L, C, o, b, lim = parts(rng)
    base = rng.integers(2, 254, (1, 8, 16, 1))
    m = np.where(rng.random((N, 8, 1, W)) < 0.06, M + rng.integers(0, 2, (N, 8, 1, W)), rng.choice(np.array([M - 1, M - 1, M - 2, 0]), (N, 8, 1, W)))
    up = np.argsort(rng.random((N, 8, 16, W)), axis=2) < m
    p = base + np.where(m == 0, 0, np.where(up, 1, 0 - rng.integers(0, 2, (N, 8, 16, W))))
    y = base + np.where(rng.random((N, 8, 1, Q)) < 0.6, 0, rng.integers(-1, 2, (N, 8, 16, Q)))
    b = rng.integers(0, 3, (N, 8, 16, Q))
    p[..., :80] = (np.arange(80).reshape(1, 80) + np.arange(16).reshape(16, 1)) >> 4
    y[..., Q - 16:] = 255; L[..., Q - 16:] = rng.integers(0, 80, (N, 8, 16, 16)); L[..., Q - 8:] = rng.integers(0, 2, (N, 8, 16, 8))
    L[:, :, 0, Q - 16:] = 0; L[:, :, 15, Q - 8:] = 1
    us = np.arange(2048, 4081 - M).reshape(-1, 1); names = np.arange(2048, W).reshape(1, -1); x = us * names
    iu, ia = np.nonzero(((x & 63) == 32) & (x > 2 ** 23) & ((((x >> 5) + names + 97) & 255) == 0) & ((names & 255) < Q - 16))
    if len(iu) > 0:
        for g in range(8):
            s = int(rng.integers(0, len(iu))); u = int(us[iu[s], 0]); a = int(names[0, ia[s]]); c = a & 255
            p[:, g, :, a] = 255; y[:, g, :, c] = (u + np.argsort(rng.random((N, 16)), axis=1)) >> 4
            C[:, g, :, c] = -1; C[:, g, 0, c] = a; o[:, g, 0, c] = 0; b[:, g, 0, c] = 7
    return pack(p, y, L, C, o, b, lim)
def setup_inputs_alike(rng):
    p, y, L, C, o, b, lim = parts(rng); c = np.arange(Q).reshape(1, 1, 1, Q)
    few = np.array([0, W - 1, W // 2, 3])
    L[:, 0::4] = rng.choice(few, (N, 2, 16, Q))
    L[:, 1::4] = np.repeat(L[:, 1::4, :1], 16, axis=2)
    L[:, 2::4] = 256 * rng.integers(0, W // 256, (N, 2, 16, Q)) + c
    L[:, 3::4] = 256 * rng.integers(0, W // 256, (N, 2, 16, Q)) + (c + 1) % Q
    own = rng.random((N, 8, 1, Q)) < 0.5
    C = np.where((C >= 0) & own, L[:, :, ::-1], C); b[:, ::2] = 2
    return pack(p, y, L, C, o, b, lim)
def check_inputs(d):
    bad = []
    for k, lo, hi in (("prop", 0, 255), ("lem", 0, W - 1), ("con", -1, W - 1), ("org", 0, 15), ("cnt", 0, 7), ("ex", 0, 255), ("lim", 0, 3)):
        a = np.asarray(d[k]).astype(np.float64)
        if not (np.min(a) >= lo and np.max(a) <= hi): bad.append("range of " + k)
        elif not np.all(a == np.floor(a)): bad.append("whole numbers in " + k)
    return bad
def pick(p, a):
    return np.take_along_axis(p, a.reshape(N, 8, 1, 16 * Q), 3).reshape(N, 8, 16, 16, Q)
def at(a, k):
    return np.take_along_axis(a, k[:, :, None, :], 2)[:, :, 0]
def reference(prop, lem, con, org, cnt, ex, lim):
    p = prop.astype(np.float32).astype(np.int16).reshape(N, 8, 16, W); y = ex.astype(np.float32).astype(np.int16).reshape(N, 8, 16, Q)
    L = lem.astype(np.int64).reshape(N, 8, 16, Q); C = con.astype(np.int64).reshape(N, 8, 16, Q)
    o = org.astype(np.float32).astype(np.int64).reshape(N, 8, 16, Q); b = cnt.astype(np.float32).astype(np.int64).reshape(N, 8, 16, Q)
    lm = lim.astype(np.int64).reshape(N, 8, 16, TV); w = np.zeros((N, Q), np.int64)
    rows = np.arange(16).reshape(1, 1, 16, 1); lane = np.arange(Q).reshape(1, 1, Q)
    for t in range(TV):
        y5 = y[:, :, :, None, :]; pl = pick(p, L); pc = pick(p, np.maximum(C, 0))
        bar = (np.add.reduce(pc > y5, axis=2, dtype=np.int64) >= M) & (C >= 0)
        gui = np.add.reduce(pl > y5, axis=2, dtype=np.int64) >= M
        score = np.add.reduce(np.abs(pl - y5), axis=2, dtype=np.int64); u = np.add.reduce(y, axis=2, dtype=np.int64)
        barred = np.any(bar, axis=2); some = np.any(gui, axis=2); guilty = ~barred & some; clear = ~barred & ~some
        kb = np.argmax(bar, axis=2); hit = barred[:, :, None] & (rows == kb[:, :, None]); b1 = b + hit
        over = hit & (b1 > lm[:, :, :, t:t + 1] + w[:, None, None, :]); back = np.any(over, axis=2)
        L1 = np.where(back[:, :, None] & (rows == at(o, kb)[:, :, None]), at(C, kb)[:, :, None], L)
        C1 = np.where(over, -1, C); b1 = np.where(over, 0, b1)
        kg = np.argmax(gui, axis=2); old = at(L, kg); empty = C < 0
        slot = np.where(np.any(empty, axis=2), np.argmax(empty, axis=2), np.argmax(b, axis=2)); put = guilty[:, :, None] & (rows == slot[:, :, None])
        n = ((((u * old) >> 5) + old + 97 * t) & (W - 256)) + lane
        C1 = np.where(put, old[:, :, None], C1); o1 = np.where(put, kg[:, :, None], o); b1 = np.where(put, 0, b1)
        L1 = np.where(guilty[:, :, None] & (rows == kg[:, :, None]), n[:, :, None], L1)
        pv = np.take_along_axis(pl, kg[:, :, None, None, :], 3)[:, :, :, 0]
        np.put_along_axis(p, n[:, :, None, :], np.where(guilty[:, :, None], np.minimum(pv, y), np.take_along_axis(p, n[:, :, None, :], 3)), 3)
        y = np.where(guilty[:, :, None], np.abs(y - pv), y)
        ks = np.argmin(score, axis=2); new = (((u * u) >> 5) + 37 * u + t) & (W - 1)
        L1 = np.where(clear[:, :, None] & (rows == ks[:, :, None]), new[:, :, None], L1)
        w = np.add.reduce(barred, axis=1, dtype=np.int64) & 3
        L, C, o, b = L1, C1, o1, b1
        if t < TV - 1: L, C, o, b = [np.roll(a, HOP, axis=0) for a in (L, C, o, b)]
    def half(a): return a.reshape(N, 128, -1).astype(np.float32).astype(BF)
    return {"zp": half(p), "zl": L.reshape(N, 128, Q).astype(np.float32), "zc": C.reshape(N, 128, Q).astype(np.float32), "zo": half(o), "zb": half(b), "zy": half(y)}

@@ -1,0 +1,514 @@
+from concourse.mybir import dt, AluOpType, AxisListType, ActivationFunctionType
+import comms_topo
+
+NV = 8
+PW = 16 + 4096 + 256
+
+SCRATCH = {
+    "pt": ("sbuf", [128, PW], "bfloat16"),
+    "ys": ("sbuf", [128, 256], "bfloat16"),
+    "yr": ("sbuf", [128, 4096], "bfloat16"),
+    "dd": ("sbuf", [128, 4096], "bfloat16"),
+    "ab": ("sbuf", [128, 4096], "bfloat16"),
+    "sg": ("sbuf", [128, 4096], "bfloat16"),
+    "cb": ("sbuf", [128, 4096], "bfloat16"),
+    "lemr": ("sbuf", [128, 256], "int32"),
+    "conr": ("sbuf", [128, 256], "int32"),
+    "orgr": ("sbuf", [128, 256], "bfloat16"),
+    "cntr": ("sbuf", [128, 256], "bfloat16"),
+    "limr": ("sbuf", [128, 8], "int32"),
+    "ll": ("sbuf", [128, 256 * NV], "uint16"),
+    "cl": ("sbuf", [128, 256 * NV], "uint16"),
+    "ls": ("sbuf", [128, 256 * NV], "float32"),
+    "xs": ("sbuf", [128, 256 * NV], "float32"),
+    "llo": ("sbuf", [128, 256 * NV], "uint16"),
+    "clo": ("sbuf", [128, 256 * NV], "uint16"),
+    "lso": ("sbuf", [128, 256 * NV], "float32"),
+    "xso": ("sbuf", [128, 256 * NV], "float32"),
+    "onf": ("sbuf", [128, 256], "float32"),
+    "idf": ("sbuf", [128, 128], "float32"),
+    "id2": ("sbuf", [128, 256], "bfloat16"),
+    "gsf": ("sbuf", [128, 8], "float32"),
+    "gst": ("sbuf", [128, 8], "float32"),
+    "gw": ("sbuf", [128, 32], "bfloat16"),
+    "k2f": ("sbuf", [128, 256], "float32"),
+    "k2b": ("sbuf", [128, 256], "bfloat16"),
+    "oneb": ("sbuf", [128, 128], "bfloat16"),
+    "cr": ("sbuf", [128, 768], "bfloat16"),
+    "mki": ("sbuf", [128, 256], "int32"),
+    "mkj": ("sbuf", [128, 256], "int32"),
+    "mk": ("sbuf", [128, 256], "float32"),
+    "rs": ("sbuf", [128, 256], "float32"),
+    "rst": ("sbuf", [128, 256], "float32"),
+    "rzb": ("sbuf", [128, 256], "bfloat16"),
+    "rzf": ("sbuf", [128, 256], "float32"),
+    "srl": ("sbuf", [128, 256], "bfloat16"),
+    "srx": ("sbuf", [128, 256], "bfloat16"),
+    "svl": ("sbuf", [128, 256], "float32"),
+    "svx": ("sbuf", [128, 256], "float32"),
+    "sz": ("sbuf", [128, 256], "float32"),
+    "kpi": ("sbuf", [128, 16], "int32"),
+    "kpa": ("sbuf", [128, 16], "int32"),
+    "ici": ("sbuf", [128, 16], "int32"),
+    "cgp": ("sbuf", [128, 16], "int32"),
+    "cc": ("sbuf", [128, 16], "int32"),
+    "lmi": ("sbuf", [128, 32], "int32"),
+    "lmf": ("sbuf", [128, 24], "float32"),
+    "dg0": ("sbuf", [128, 256], "bfloat16"),
+    "dg1": ("sbuf", [128, 256], "bfloat16"),
+    "fa": ("sbuf", [128, 256], "float32"),
+    "fb": ("sbuf", [128, 256], "float32"),
+    "fc": ("sbuf", [128, 256], "float32"),
+    "xsi": ("sbuf", [128, 256], "int32"),
+    "xsf": ("sbuf", [128, 256], "int32"),
+    "sk": ("sbuf", [128, 256], "float32"),
+    "sm": ("sbuf", [128, 256], "float32"),
+    "xk": ("sbuf", [128, 256], "float32"),
+    "lk": ("sbuf", [128, 256], "float32"),
+    "kg": ("sbuf", [128, 256], "float32"),
+    "qq": ("sbuf", [128, 256], "float32"),
+    "key": ("sbuf", [128, 256], "float32"),
+    "pm": ("sbuf", [128, 256], "float32"),
+    "ra": ("sbuf", [128, 256], "bfloat16"),
+    "ma": ("sbuf", [128, 256], "bfloat16"),
+    "rb": ("sbuf", [128, 256], "bfloat16"),
+    "mb": ("sbuf", [128, 256], "bfloat16"),
+    "zx": ("sbuf", [128, 256], "float32"),
+    "pi": ("sbuf", [128, 16 * 40], "int32"),
+    "pl": ("sbuf", [128, 16 * 40], "float32"),
+    "wj": ("sbuf", [128, 16], "float32"),
+    "ws": ("sbuf", [128, 16], "float32"),
+    "wi": ("sbuf", [128, 16], "int32"),
+    "wk": ("sbuf", [128, 16], "int32"),
+    "wf": ("sbuf", [128, 16], "float32"),
+    "aof": ("sbuf", [128, 16], "uint16"),
+    "nof": ("sbuf", [128, 16], "uint16"),
+    "ee": ("sbuf", [128, 256], "bfloat16"),
+    "mn": ("sbuf", [128, 256], "bfloat16"),
+    "ofl": ("sbuf", [128, 256], "float32"),
+    "ofc": ("sbuf", [128, 256], "float32"),
+    "obo": ("sbuf", [128, 256], "bfloat16"),
+    "obb": ("sbuf", [128, 256], "bfloat16"),
+    "oi": ("sbuf", [128, 768], "int32"),
+    "pb": ("psum", [128, 512], "float32"),
+    "pg": ("psum", [128, 512], "float32"),
+    "pk": ("psum", [128, 512], "float32"),
+    "pcn": ("psum", [128, 512], "float32"),
+    "pe": ("psum", [128, 512], "float32"),
+    "pf": ("psum", [128, 512], "float32"),
+    "px": ("psum", [128, 512], "float32"),
+    "ph": ("psum", [128, 512], "float32"),
+}
+PSUM = ("pb", "pg", "pk", "pcn", "pe", "pf", "px", "ph")
+SEMAPHORES = (["sv", "ss", "st", "sp", "loc"] + ["i%d" % i for i in range(7)] + ["o%d" % i for i in range(6)]
+              + ["%s%d" % (a, t) for a in ("al", "ac", "as", "ax") for t in range(1, NV)])
+
+
+def rank_program(g, core, T, topo):
+    rank = T.rank_of(core)
+    if rank is None:
+        return
+    n = len(T.cores)
+    nxt, prv = T.cores[(rank + 1) % n], T.cores[(rank - 1) % n]
+    Op = AluOpType
+    F = ActivationFunctionType
+    queue = {"v": g.vector, "s": g.scalar, "t": g.tensor, "p": g, "y": g.sync}
+    own = {"v": "sv", "s": "ss", "t": "st", "p": "sp"}
+    count = {"v": 0, "s": 0, "t": 0, "p": 0}
+    known = {q: {} for q in queue}
+    wrote, readers, touched = {}, {}, {}
+
+    def A(name, lo=None, hi=None, step=None, key=None):
+        t = T[name]
+        ap = t[:, :] if lo is None else (t[:, lo:hi] if step is None else t[:, lo:hi:step])
+        return (ap, ((name, key),))
+
+    def need(q, reads, writes, selfok):
+        want = {}
+
+        def add(tok, free=False):
+            if free and tok[0] == own.get(q):
+                return
+            if want.get(tok[0], 0) < tok[1]:
+                want[tok[0]] = tok[1]
+        for k in reads:
+            for tok in wrote.get(k, ()):
+                add(tok)
+        for k in writes:
+            for tok in wrote.get(k, ()):
+                add(tok, selfok)
+            for tok in readers.get(k, {}).items():
+                add(tok, selfok)
+        for k in list(reads) + list(writes):
+            if k[0] in PSUM:
+                for e, tok in touched.get(k[0], {}).items():
+                    if e != q:
+                        add(tok)
+        for s, v in want.items():
+            if known[q].get(s, 0) < v:
+                queue[q].wait_ge(T.sem[s], v)
+                known[q][s] = v
+
+    def note(q, tok, reads, writes):
+        for k in writes:
+            wrote[k] = [tok]
+            readers[k] = {}
+        for k in reads:
+            r = readers.setdefault(k, {})
+            r[tok[0]] = max(r.get(tok[0], 0), tok[1])
+        for k in list(reads) + list(writes):
+            if k[0] in PSUM:
+                touched.setdefault(k[0], {})[q] = tok
+
+    def op(q, call, outs, ins, selfok=False):
+        reads = [k for o in ins for k in o[1]]
+        writes = [k for o in outs for k in o[1]]
+        need(q, reads, writes, selfok)
+        count[q] += 1
+        call().then_inc(T.sem[own[q]], 1)
+        note(q, (own[q], count[q]), reads, writes)
+
+    def tt(o, a, b, f):
+        op("v", lambda: g.vector.tensor_tensor(o[0], a[0], b[0], f), [o], [a, b])
+
+    def ts(o, a, s1, f1, s2=None, f2=None):
+        col = [s1] if isinstance(s1, tuple) else []
+        x = s1[0] if col else s1
+        if f2 is None:
+            op("v", lambda: g.vector.tensor_scalar(o[0], a[0], x, None, f1), [o], [a] + col)
+        else:
+            op("v", lambda: g.vector.tensor_scalar(o[0], a[0], x, s2, f1, f2), [o], [a] + col)
+
+    def cp(o, a):
+        op("v", lambda: g.vector.tensor_copy(o[0], a[0]), [o], [a])
+
+    def ms(o, c):
+        op("v", lambda: g.vector.memset(o[0], c), [o], [])
+
+    def scan(o, d0, d1, init, f0, f1):
+        op("v", lambda: g.vector.tensor_tensor_scan(o[0], d0[0], d1[0], init, f0, f1), [o], [d0, d1])
+
+    def act(o, a, f, bias=0.0, acc=None):
+        if acc is None:
+            op("s", lambda: g.scalar.activation(o[0], a[0], f, bias=bias), [o], [a])
+        else:
+            op("s", lambda: g.scalar.activation(o[0], a[0], f, accum_out=acc[0]), [o, acc], [a])
+
+    def mm(o, l, r, start, stop):
+        op("t", lambda: g.tensor.matmul(o[0], l[0], r[0], start, stop), [o], [l, r], selfok=True)
+
+    def turn(o, a):
+        i = A("idf")
+        op("t", lambda: g.tensor.transpose(o[0], a[0], i[0]), [o], [a, i], selfok=True)
+
+    def dma(q, o, a, sem, okeys, ikeys):
+        need(q, ikeys, okeys, False)
+        queue[q].dma_start(o, a).then_inc(T.sem[sem], 16)
+        note(q, (sem, 16), ikeys, okeys)
+
+    def ind(name, lo, hi, off, olo, ohi, okey):
+        return (T[name][:, lo:hi].indirect(T[off][:, olo:ohi]), ((name, None), (off, okey)))
+
+    dma("y", T.lemr[:, :], T.lem[:, :], "i0", [("lemr", None)], [])
+    dma("s", T.ys[:, :], T.ex[:, :], "i1", [("ys", None)], [])
+    dma("s", T.pt[:, 16:4112], T.prop[:, :], "i2", [("pt", None)], [])
+    dma("y", T.conr[:, :], T.con[:, :], "i3", [("conr", None)], [])
+    dma("y", T.cntr[:, :], T.cnt[:, :], "i4", [("cntr", None)], [])
+    dma("y", T.orgr[:, :], T.org[:, :], "i5", [("orgr", None)], [])
+    dma("y", T.limr[:, :], T.lim[:, :], "i6", [("limr", None)], [])
+
+    op("v", lambda: g.vector.memset(T.pt[:, 0:16], 0.0), [(None, (("ptz", None),))], [])
+    ms(A("onf"), 1.0)
+
+    def p_iota(o, pattern, base, cm, flag):
+        if flag:
+            op("p", lambda: g.iota(o[0], pattern, base, cm, allow_small_or_imprecise_dtypes=True), [o], [])
+        else:
+            op("p", lambda: g.iota(o[0], pattern, base, cm), [o], [])
+
+    def p_sel(o, a, pattern, f, base, cm):
+        op("p", lambda: g.affine_select(o[0], a[0], pattern, f, 0.0, base, cm), [o], [a])
+    p_iota(A("k2f"), [[0, 16], [2, 16]], 0, 0, True)
+    p_sel(A("gst"), A("onf", 0, 8), [[-16, 8]], Op.is_ge, 0, 1)
+    p_sel(A("gsf"), A("gst"), [[16, 8]], Op.is_ge, 15, -1)
+    p_sel(A("idf"), A("onf", 0, 128), [[-1, 128]], Op.is_equal, 0, 1)
+    p_iota(A("kpa"), [[0, 16]], 0, 1, False)
+    p_iota(A("ici"), [[16, 16]], 0, 0, False)
+    p_iota(A("cc"), [[128, 2], [0, 8]], 0, 1, False)
+    p_iota(A("mki"), [[0, 16], [-1, 16]], 0, 1, False)
+
+    cp(A("ll", 0, 256, key=0), A("lemr"))
+
+    def spread(h):
+        for k in range(16):
+            o, a = A("yr", 2048 * h + k, 2048 * h + 2048, 16, key=h), A("ys", 128 * h, 128 * h + 128)
+            op("s", lambda: g.scalar.activation(o[0], a[0], F.Copy), [o], [a], selfok=True)
+    spread(0)
+    spread(1)
+
+    ms(A("oneb"), 1.0)
+    ms(A("cr", 0, 256, key=0), float(17 * 2 ** 25))
+    ms(A("cr", 256, 512, key=1), float(2 ** 25))
+    ms(A("cr", 512, 768, key=2), float(9 * 2 ** 21))
+    ms(A("srl"), -2.0)
+    ms(A("srx"), -2.0)
+    ms(A("svl"), 0.0)
+    ms(A("svx"), 0.0)
+    ms(A("sz"), 0.0)
+    for i, wgt in enumerate((1.0, 32.0, float(-2 ** 25), float(-2 ** 26))):
+        ts(A("gw", 8 * i, 8 * i + 8, key=i), A("gsf"), wgt, Op.mult)
+    cp(A("k2b"), A("k2f"))
+    cp(A("id2", 0, 128, key=0), A("idf"))
+    cp(A("id2", 128, 256, key=1), A("idf"))
+    ID2 = (T.id2[:, :], (("id2", 0), ("id2", 1)))
+    ONE1 = (T.oneb[0:1, :], (("oneb", None),))
+
+    def constants():
+        ts(A("mkj"), A("mki"), 15, Op.bitwise_and)
+        ts(A("mk"), A("mkj"), 0.0, Op.is_equal)
+        ts(A("rst"), A("k2f"), 0.0, Op.is_equal, 2.0e9, Op.mult)
+        ts(A("rs"), A("rst"), -1.0e9, Op.add)
+        ts(A("rzb"), A("k2f"), 0.0, Op.is_gt)
+        ts(A("rzf"), A("k2f"), 0.0, Op.is_gt)
+        cp(A("pcn", 0, 256, key=0), A("k2f"))
+        ts(A("pcn", 256, 512, key=1), A("k2f"), 65537.0, Op.mult, 16777216.0, Op.add)
+        ts(A("kpi"), A("kpa"), 15, Op.bitwise_and)
+        tt(A("cgp"), A("kpi"), A("ici"), Op.add)
+        ts(A("lmi", 0, 8, key=0), A("limr"), 1, Op.bitwise_and)
+        ts(A("lmi", 8, 16, key=1), A("limr"), 1, Op.arith_shift_right)
+        ts(A("lmi", 16, 24, key=2), A("kpi", 0, 8), 2.0, Op.mult, -16.0, Op.add)
+        cp(A("lmf", 0, 8, key=0), A("lmi", 0, 8, key=0))
+        tt(A("lmf", 8, 16, key=1), A("lmi", 8, 16, key=1), A("lmi", 16, 24, key=2), Op.add)
+        ts(A("lmf", 16, 24, key=2), A("lmf", 8, 16, key=1), float(2 ** 20), Op.mult)
+
+    def first_state():
+        ts(A("fa"), A("lemr"), 32.0, Op.mult)
+        for h in range(2):
+            turn(A("pf", 128 * h, 128 * h + 128, key="l"), A("fa", 128 * h, 128 * h + 128))
+        cp(A("ls", 0, 256, key=0), A("pf", 0, 256, key="l"))
+        ts(A("fb"), A("conr"), 256.0, Op.mult)
+        ts(A("fc"), A("cntr"), 32.0, Op.mult)
+        tt(A("sk"), A("fb"), A("fc"), Op.add)
+        ts(A("fc"), A("orgr"), 2.0, Op.mult)
+        tt(A("fb"), A("sk"), A("fc"), Op.add)
+        for h in range(2):
+            turn(A("px", 128 * h, 128 * h + 128, key="x"), A("fb", 128 * h, 128 * h + 128))
+        cp(A("xs", 0, 256, key=0), A("px", 0, 256, key="x"))
+
+    def I(j, key=None):
+        return A("pi", 16 * j, 16 * j + 16, key=j)
+
+    def L(j):
+        return A("pl", 16 * j, 16 * j + 16, key=j)
+
+    rid, pid, _ = topo.addr(nxt)
+    mask = topo.mask(core, nxt)
+    n_in = len(topo.engines(prv, core))
+    n_out = len(topo.engines(core, nxt))
+    sent = [0]
+
+    def send(src, dst, sem, t):
+        need("p", [(src, t)], [], False)
+        g.remote_dma(T[dst][:, 256 * (t + 1):256 * (t + 2)], T[src][:, 256 * t:256 * (t + 1)],
+                     T.sem["%s%d" % (sem, t + 1)], T.sem.loc, pid, rid, mask)
+        sent[0] += n_out
+        wrote[(dst, t + 1)] = [("%s%d" % (sem, t + 1), n_in)]
+
+    for t in range(NV):
+        c0 = 256 * t
+        last = t == NV - 1
+        mm(A("pg", 0, 256), ONE1, (T.cr[0:1, 256:512], (("cr", 1),)), True, False)
+        mm(A("pk", 0, 256), ONE1, (T.cr[0:1, 512:768], (("cr", 2),)), True, False)
+        mm(A("pk", 0, 256), ONE1, (T.k2b[0:1, :], (("k2b", None),)), False, False)
+        mm(A("pb", 0, 256), ONE1, (T.cr[0:1, 0:256], (("cr", 0),)), True, False)
+        for h in range(2):
+            mm(A("pe", 256 + 8 * h, 264 + 8 * h, key="u"), A("ys", 128 * h, 128 * h + 128), A("gw", 0, 8, key=0), True, True)
+
+        for q in range(4):
+            h, lo = q // 2, 1024 * q
+            tt(A("dd", lo, lo + 1024, key=q), ind("pt", 16, 4112, "ll", c0 + 64 * q, c0 + 64 * q + 64, t),
+               A("yr", lo, lo + 1024, key=h), Op.subtract)
+            act(A("ab", lo, lo + 1024, key=q), A("dd", lo, lo + 1024, key=q), F.Abs)
+            act(A("sg", lo, lo + 1024, key=q), A("dd", lo, lo + 1024, key=q), F.Sign, bias=-0.5)
+            if q % 2 == 1:
+                for k in range(16):
+                    two = (("ab", q - 1), ("ab", q))
+                    mm(A("pk", 128 * h + k, 128 * h + 128, 16), (T.ab[:, 2048 * h + k:2048 * h + 2048:16], two),
+                       A("gw", 8, 16, key=1), False, q == 3 and k == 15)
+                for k in range(16):
+                    two = (("sg", q - 1), ("sg", q))
+                    mm(A("pg", 128 * h + k, 128 * h + 128, 16), (T.sg[:, 2048 * h + k:2048 * h + 2048:16], two),
+                       A("gw", 16, 24, key=2), False, q == 3 and k == 15)
+        if t == 0:
+            ts(A("cl", 0, 256, key=0), A("conr"), 16.0, Op.add)
+        for q in range(4):
+            h, lo = q // 2, 1024 * q
+            w = ind("pt", 0, 4112, "cl", c0 + 64 * q, c0 + 64 * q + 64, t)
+            tt(A("cb", lo, lo + 1024, key=q), (w[0], w[1] + (("ptz", None),)), A("yr", lo, lo + 1024, key=h), Op.is_gt)
+            if q % 2 == 1:
+                for k in range(16):
+                    two = (("cb", q - 1), ("cb", q))
+                    mm(A("pb", 128 * h + k, 128 * h + 128, 16), (T.cb[:, 2048 * h + k:2048 * h + 2048:16], two),
+                       A("gw", 24, 32, key=3), False, q == 3 and k == 15)
+        if t == 0:
+            constants()
+            first_state()
+        LS, XS = A("ls", c0, c0 + 256, key=t), A("xs", c0, c0 + 256, key=t)
+        ts(A("dg0"), ID2, A("lmf", t, t + 1, key=0), Op.mult)
+        ts(A("dg1"), ID2, A("lmf", 16 + t, 17 + t, key=2), Op.mult)
+        ALL = A("oneb")
+        mm(A("pe", 0, 256, key="l"), ALL, A("dg0"), True, False)
+        mm(A("pe", 0, 256, key="l"), ALL, A("dg1"), False, True)
+        cp(A("xsi"), XS)
+        ts(A("xsf"), A("xsi"), 0x1000E0, Op.bitwise_and)
+        ts(A("sm"), A("xsf"), 256.0, Op.min, -1.0, Op.mult)
+        tt(A("sk"), A("pcn", 0, 256, key=0), A("sm"), Op.add)
+        scan(A("sm"), A("rs"), A("sk"), 1.0e9, Op.max, Op.min)
+        cp(I(0), A("sm", 15, 256, 16))
+        ts(I(1), I(0), 30, Op.bitwise_and)
+        U = L(0)
+        cp(U, A("pe", 256, 272, key="u"))
+        tt(I(2), U, U, Op.mult)
+        ts(I(3), I(2), 5, Op.arith_shift_right)
+        ts(I(4), U, 37.0, Op.mult, float(t), Op.add)
+        tt(I(5), I(3), I(4), Op.add)
+        ts(I(6), I(5), 4095, Op.bitwise_and)
+        tt(A("lk"), A("pcn", 256, 512, key=1), LS, Op.add)
+        tt(A("xk"), A("pe", 0, 256, key="l"), XS, Op.add)
+        tt(A("kg"), A("pg", 0, 256), A("lk"), Op.max)
+        tt(A("qq"), A("pk", 0, 256), A("kg"), Op.min)
+        tt(A("ph", 0, 256, key=0), A("pb", 0, 256), A("xk"), Op.max)
+        tt(A("key"), A("ph", 0, 256, key=0), A("qq"), Op.min)
+        scan(A("pm"), A("rs"), A("key"), 1.0e9, Op.max, Op.min)
+        M = I(7)
+        cp(M, A("pm", 15, 256, 16))
+        a, j = I(8), I(9)
+        B32, CL32, NB32, G32 = L(1), L(2), L(3), L(4)
+        ts(a, M, 5, Op.arith_shift_right, 4095, Op.bitwise_and)
+        ts(NB32, M, 16777216.0, Op.is_ge, 32.0, Op.mult)
+        ts(CL32, M, 16777216.0 + 2097152.0, Op.is_ge, 32.0, Op.mult)
+        ts(B32, M, 16777216.0, Op.is_lt, 32.0, Op.mult)
+        tt(I(10), U, a, Op.mult)
+        ts(I(11), a, float(97 * t), Op.add)
+        tt(G32, NB32, CL32, Op.subtract)
+        ts(I(12), I(10), 5, Op.arith_shift_right)
+        ts(I(14), M, 5, Op.arith_shift_right, 7, Op.bitwise_and)
+        ts(I(15), M, 1, Op.bitwise_and)
+        tt(I(13), I(12), I(11), Op.add)
+        ts(I(16), M, 19, Op.arith_shift_right, 2, Op.bitwise_and)
+        ts(I(19), M, 30, Op.bitwise_and)
+        ts(j, I(13), 3840, Op.bitwise_and)
+        tt(L(5), I(15), I(16), Op.add)
+        ts(I(18), M, 8, Op.arith_shift_right, 4095, Op.bitwise_and)
+        tt(I(17), j, A("cc"), Op.add)
+        if t:
+            for h in range(2):
+                ts((T.pl[:, 96 + 8 * h:104 + 8 * h], (("pl", 6),)), (T.pl[:, 80 + 8 * h:88 + 8 * h], (("pl", 5),)),
+                   A("wf", h, h + 1), Op.add)
+            s3 = L(6)
+        else:
+            s3 = L(5)
+        tt(L(8), I(18), B32, Op.mult)
+        tt(L(9), I(6), CL32, Op.mult)
+        tt(L(7), I(14), s3, Op.is_lt)
+        tt(L(10), I(17), G32, Op.mult)
+        tt(L(11), L(8), L(9), Op.add)
+        tt(L(12), L(7), B32, Op.mult)
+        tt(A("svl", 0, 256, 16), L(11), L(10), Op.add)
+        tt(A("srl", 0, 256, 16), L(12), I(19), Op.add)
+        scan(A("ph", 0, 256, key=0), A("rzf"), A("svl"), 0.0, Op.mult, Op.add)
+        scan(A("ra"), A("rzb"), A("srl"), 0.0, Op.mult, Op.add)
+        tt(A("ph", 256, 512, key=1), A("ph", 0, 256, key=0), LS, Op.subtract)
+        ts(A("ma"), A("ra"), 0.0, Op.is_equal)
+        LO = A("lso", c0, c0 + 256, key=t)
+        tt(A("ph", 0, 256, key=0), A("ph", 256, 512, key=1), A("ma"), Op.mult)
+        ts(I(20), M, 21, Op.arith_shift_right)
+        ts(I(23), M, 0xFFFE0, Op.bitwise_and)
+        tt(LO, A("ph", 0, 256, key=0), LS, Op.add)
+        for h in range(2):
+            turn(A("pf", 128 * h, 128 * h + 128, key="l"), A("lso", c0 + 128 * h, c0 + 128 * h + 128, key=t))
+        ts(L(14), I(20), 2.0, Op.mult, 16.0, Op.add)
+        ts(L(15), M, 16777216.0, Op.is_lt)
+        tt(L(16), L(14), I(1), Op.subtract)
+        ts(L(20), I(23), 1.0 / 32, Op.mult, 1.0, Op.add)
+        tt(L(17), L(16), L(15), Op.mult)
+        tt(L(21), L(20), L(12), Op.mult)
+        tt(L(18), L(17), I(1), Op.add)
+        tt(L(22), B32, L(12), Op.subtract)
+        tt(L(23), a, G32, Op.mult)
+        tt(A("srx", 0, 256, 16), L(18), CL32, Op.add)
+        tt(L(24), L(23), L(22), Op.subtract)
+        tt(L(26), L(21), I(19), Op.add)
+        ts(L(25), L(24), 8.0, Op.mult)
+        if not last:
+            ts(A("llo", c0, c0 + 256, key=t), A("pf", 0, 256, key="l"), 1.0 / 32, Op.mult)
+            send("llo", "ll", "al", t)
+        tt(A("svx", 0, 256, 16), L(25), L(26), Op.add)
+        scan(A("rb"), A("rzb"), A("srx"), 0.0, Op.mult, Op.add)
+        scan(A("ph", 0, 256, key=0), A("rzf"), A("svx"), 0.0, Op.mult, Op.add)
+        ts(A("mb"), A("rb"), 0.0, Op.is_equal)
+        tt(A("ph", 256, 512, key=1), A("ph", 0, 256, key=0), XS, Op.subtract)
+        ts(L(28), j, -4096.0, Op.add, 1.0 / 8192, Op.mult)
+        tt(A("ph", 0, 256, key=0), A("ph", 256, 512, key=1), A("mb"), Op.mult)
+        tt(L(29), L(23), G32, Op.add)
+        tt(A("xso", c0, c0 + 256, key=t), A("ph", 0, 256, key=0), XS, Op.add)
+        for h in range(2):
+            turn(A("px", 128 * h, 128 * h + 128, key="x"), A("xso", c0 + 128 * h, c0 + 128 * h + 128, key=t))
+        tt(L(30), L(28), G32, Op.mult)
+        tt(A("sz", 0, 256, 16), L(30), L(29), Op.add)
+        scan(A("ph", 0, 256, key=0), A("rzf"), A("sz"), 0.0, Op.mult, Op.add)
+        tt(A("zx"), A("ph", 0, 256, key=0), A("mk"), Op.mult)
+        for h in range(2):
+            mm(A("pe", 272 + 8 * h, 280 + 8 * h, key="z"), A("zx", 128 * h, 128 * h + 128), A("gsf"), True, True)
+        if not last:
+            ts(A("clo", c0, c0 + 256, key=t), A("px", 0, 256, key="x"), 1.0 / 256, Op.mult, 15.502, Op.add)
+            send("clo", "cl", "ac", t)
+            send("xso", "xs", "ax", t)
+            send("lso", "ls", "as", t)
+            for h in range(2):
+                op("s", lambda: g.scalar.activation(T.wj[:, 8 * h:8 * h + 8], T.pl[:, 16 + 8 * h:24 + 8 * h], F.Copy,
+                                                    accum_out=T.ws[:, h:h + 1]),
+                   [A("wj", key=h), A("ws", key=h)], [B32])
+        ts(I(24), A("pe", 272, 288, key="z"), 16.0, Op.add)
+        ts(I(25), I(24), 5, Op.arith_shift_right)
+        ts(I(26), I(24), 31, Op.bitwise_and)
+        ts(A("aof"), I(25), 15.0, Op.add)
+        ts(I(27), I(26), 256.0, Op.mult)
+        w = ind("pt", 0, 4112, "aof", 0, 16, None)
+        w = (w[0], w[1] + (("ptz", None),))
+        Y = A("ys")
+        tt(A("ee"), w, Y, Op.subtract)
+        tt(I(28), I(27), A("cgp"), Op.add)
+        tt(A("mn"), w, Y, Op.min)
+        cp(A("nof"), I(28))
+        act(Y, A("ee"), F.Abs)
+        op("v", lambda: g.vector.tensor_copy(T.pt[:, 16:PW].indirect(T.nof[:, 0:16]), T.mn[:, :]),
+           [A("pt")], [A("mn"), A("nof")])
+        if not last:
+            spread(0)
+            spread(1)
+            cpw = (T.ws[:, 0:2], (("ws", 0), ("ws", 1)))
+            ts(A("wi", 0, 2), cpw, 1.0 / 32, Op.mult)
+            ts(A("wk", 0, 2), A("wi", 0, 2), 3, Op.bitwise_and)
+            cp(A("wf", 0, 2), A("wk", 0, 2))
+
+    dma("y", T.zp[:, :], T.pt[:, 16:4112], "o0", [("zp", None)], [("pt", None)])
+    dma("s", T.zy[:, :], T.ys[:, :], "o1", [("zy", None)], [("ys", None)])
+    ts(A("ofl"), A("pf", 0, 256, key="l"), 1.0 / 32, Op.mult)
+    dma("y", T.zl[:, :], T.ofl[:, :], "o2", [("zl", None)], [("ofl", None)])
+    cp(A("xsi"), A("px", 0, 256, key="x"))
+    ts(A("oi", 0, 256, key=0), A("xsi"), 8, Op.arith_shift_right)
+    ts(A("oi", 256, 512, key=1), A("xsi"), 1, Op.arith_shift_right, 15, Op.bitwise_and)
+    ts(A("oi", 512, 768, key=2), A("xsi"), 5, Op.arith_shift_right, 7, Op.bitwise_and)
+    cp(A("ofc"), A("oi", 0, 256, key=0))
+    dma("y", T.zc[:, :], T.ofc[:, :], "o3", [("zc", None)], [("ofc", None)])
+    cp(A("obo"), A("oi", 256, 512, key=1))
+    dma("s", T.zo[:, :], T.obo[:, :], "o4", [("zo", None)], [("obo", None)])
+    cp(A("obb"), A("oi", 512, 768, key=2))
+    dma("y", T.zb[:, :], T.obb[:, :], "o5", [("zb", None)], [("obb", None)])
+    for q in ("v", "s", "t", "p"):
+        if known["p"].get(own[q], 0) < count[q]:
+            g.wait_ge(T.sem[own[q]], count[q])
+    g.wait_ge(T.sem.loc, sent[0])
+    for i in range(6):
+        g.wait_ge(T.sem["o%d" % i], 16)

@@ -6,7 +6,7 @@ PW = 16 + 4096 + 256
 
 SCRATCH = {
     "pt": ("sbuf", [128, PW], "bfloat16"),
-    "ys": ("sbuf", [128, 256], "bfloat16"),
+    "ys": ("sbuf", [128, 512], "bfloat16"),
     "yr": ("sbuf", [128, 4096], "bfloat16"),
     "dd": ("sbuf", [128, 4096], "bfloat16"),
     "ab": ("sbuf", [128, 4096], "bfloat16"),
@@ -19,12 +19,10 @@ SCRATCH = {
     "limr": ("sbuf", [128, 8], "int32"),
     "ll": ("sbuf", [128, 256 * NV], "uint16"),
     "cl": ("sbuf", [128, 256 * NV], "uint16"),
-    "ls": ("sbuf", [128, 256 * NV], "float32"),
-    "xs": ("sbuf", [128, 256 * NV], "float32"),
+    "rl": ("sbuf", [128, 256 * NV], "bfloat16"),
     "llo": ("sbuf", [128, 256 * NV], "uint16"),
     "clo": ("sbuf", [128, 256 * NV], "uint16"),
-    "lso": ("sbuf", [128, 256 * NV], "float32"),
-    "xso": ("sbuf", [128, 256 * NV], "float32"),
+    "rlo": ("sbuf", [128, 256 * NV], "bfloat16"),
     "onf": ("sbuf", [128, 256], "float32"),
     "idf": ("sbuf", [128, 128], "float32"),
     "id2": ("sbuf", [128, 256], "bfloat16"),
@@ -34,19 +32,40 @@ SCRATCH = {
     "k2f": ("sbuf", [128, 256], "float32"),
     "k2b": ("sbuf", [128, 256], "bfloat16"),
     "oneb": ("sbuf", [128, 128], "bfloat16"),
-    "cr": ("sbuf", [128, 768], "bfloat16"),
-    "mki": ("sbuf", [128, 256], "int32"),
-    "mkj": ("sbuf", [128, 256], "int32"),
-    "mk": ("sbuf", [128, 256], "float32"),
+    "cr": ("sbuf", [128, 1024], "bfloat16"),
+    "mki": ("sbuf", [128, 16], "int32"),
+    "mkj": ("sbuf", [128, 16], "int32"),
+    "mk": ("sbuf", [128, 16], "float32"),
     "rs": ("sbuf", [128, 256], "float32"),
     "rst": ("sbuf", [128, 256], "float32"),
     "rzb": ("sbuf", [128, 256], "bfloat16"),
     "rzf": ("sbuf", [128, 256], "float32"),
     "srl": ("sbuf", [128, 256], "bfloat16"),
     "srx": ("sbuf", [128, 256], "bfloat16"),
-    "svl": ("sbuf", [128, 256], "float32"),
-    "svx": ("sbuf", [128, 256], "float32"),
-    "sz": ("sbuf", [128, 256], "float32"),
+    "lb": ("sbuf", [128, 2048], "bfloat16"),
+    "lkr": ("sbuf", [128, 256], "bfloat16"),
+    "lf": ("sbuf", [128, 512], "float16"),
+    "cf": ("sbuf", [128, 512], "float16"),
+    "em": ("sbuf", [128, 256], "bfloat16"),
+    "rho": ("sbuf", [128, 256], "bfloat16"),
+    "dmb": ("sbuf", [128, 128], "bfloat16"),
+    "d16": ("sbuf", [128, 256], "float16"),
+    "i16": ("sbuf", [128, 384], "float16"),
+    "oh": ("sbuf", [128, 128], "float16"),
+    "r16": ("sbuf", [128, 256], "float16"),
+    "rk0": ("sbuf", [128, 512], "float16"),
+    "xn": ("sbuf", [128, 256], "float32"),
+    "shf": ("sbuf", [128, 128], "float32"),
+    "shm": ("sbuf", [128, 128], "float32"),
+    "dmf": ("sbuf", [128, 128], "float32"),
+    "dml": ("sbuf", [128, 256], "float32"),
+    "dmx": ("sbuf", [128, 256], "float32"),
+    "ia": ("sbuf", [128, 48], "int32"),
+    "fl": ("sbuf", [128, 48], "float32"),
+    "p3": ("sbuf", [128, 48], "float32"),
+    "zz": ("sbuf", [128, 16], "float32"),
+    "smb": ("sbuf", [128, 256], "bfloat16"),
+    "w8": ("sbuf", [128, 16], "float32"),
     "kpi": ("sbuf", [128, 16], "int32"),
     "kpa": ("sbuf", [128, 16], "int32"),
     "ici": ("sbuf", [128, 16], "int32"),
@@ -54,9 +73,6 @@ SCRATCH = {
     "cc": ("sbuf", [128, 16], "int32"),
     "lmi": ("sbuf", [128, 32], "int32"),
     "lmf": ("sbuf", [128, 24], "float32"),
-    "dg0": ("sbuf", [128, 256], "bfloat16"),
-    "dg1": ("sbuf", [128, 256], "bfloat16"),
-    "fa": ("sbuf", [128, 256], "float32"),
     "fb": ("sbuf", [128, 256], "float32"),
     "fc": ("sbuf", [128, 256], "float32"),
     "xsi": ("sbuf", [128, 256], "int32"),
@@ -101,7 +117,7 @@ SCRATCH = {
 }
 PSUM = ("pb", "pg", "pk", "pcn", "pe", "pf", "px", "ph")
 SEMAPHORES = (["sv", "ss", "st", "sp", "loc"] + ["i%d" % i for i in range(7)] + ["o%d" % i for i in range(6)]
-              + ["%s%d" % (a, t) for a in ("al", "ac", "as", "ax") for t in range(1, NV)])
+              + ["%s%d" % (a, t) for a in ("al", "ac", "ar") for t in range(1, NV)])
 
 
 def rank_program(g, core, T, topo):
@@ -188,18 +204,16 @@ def rank_program(g, core, T, topo):
     def scan(o, d0, d1, init, f0, f1):
         op("v", lambda: g.vector.tensor_tensor_scan(o[0], d0[0], d1[0], init, f0, f1), [o], [d0, d1])
 
-    def act(o, a, f, bias=0.0, acc=None):
-        if acc is None:
+    def act(o, a, f, bias=0.0, acc=None, scale=None):
+        if scale is not None:
+            op("s", lambda: g.scalar.activation(o[0], a[0], f, scale=scale[0]), [o], [a, scale], selfok=True)
+        elif acc is None:
             op("s", lambda: g.scalar.activation(o[0], a[0], f, bias=bias), [o], [a])
         else:
             op("s", lambda: g.scalar.activation(o[0], a[0], f, accum_out=acc[0]), [o, acc], [a])
 
     def mm(o, l, r, start, stop):
         op("t", lambda: g.tensor.matmul(o[0], l[0], r[0], start, stop), [o], [l, r], selfok=True)
-
-    def turn(o, a):
-        i = A("idf")
-        op("t", lambda: g.tensor.transpose(o[0], a[0], i[0]), [o], [a, i], selfok=True)
 
     def dma(q, o, a, sem, okeys, ikeys):
         need(q, ikeys, okeys, False)
@@ -210,7 +224,7 @@ def rank_program(g, core, T, topo):
         return (T[name][:, lo:hi].indirect(T[off][:, olo:ohi]), ((name, None), (off, okey)))
 
     dma("y", T.lemr[:, :], T.lem[:, :], "i0", [("lemr", None)], [])
-    dma("s", T.ys[:, :], T.ex[:, :], "i1", [("ys", None)], [])
+    dma("s", T.ys[:, 0:256], T.ex[:, :], "i1", [("ys", 0)], [])
     dma("s", T.pt[:, 16:4112], T.prop[:, :], "i2", [("pt", None)], [])
     dma("y", T.conr[:, :], T.con[:, :], "i3", [("conr", None)], [])
     dma("y", T.cntr[:, :], T.cnt[:, :], "i4", [("cntr", None)], [])
@@ -235,16 +249,18 @@ def rank_program(g, core, T, topo):
     p_iota(A("kpa"), [[0, 16]], 0, 1, False)
     p_iota(A("ici"), [[16, 16]], 0, 0, False)
     p_iota(A("cc"), [[128, 2], [0, 8]], 0, 1, False)
-    p_iota(A("mki"), [[0, 16], [-1, 16]], 0, 1, False)
+    p_iota(A("mki"), [[-1, 16]], 0, 1, False)
+    p_sel(A("shf"), A("onf", 0, 128), [[-1, 128]], Op.is_equal, 1, 1)
 
     cp(A("ll", 0, 256, key=0), A("lemr"))
 
-    def spread(h):
+    def spread(h, par):
         for k in range(16):
-            o, a = A("yr", 2048 * h + k, 2048 * h + 2048, 16, key=h), A("ys", 128 * h, 128 * h + 128)
+            o = A("yr", 2048 * h + k, 2048 * h + 2048, 16, key=h)
+            a = A("ys", 256 * par + 128 * h, 256 * par + 128 * h + 128, key=par)
             op("s", lambda: g.scalar.activation(o[0], a[0], F.Copy), [o], [a], selfok=True)
-    spread(0)
-    spread(1)
+    spread(0, 0)
+    spread(1, 0)
 
     ms(A("oneb"), 1.0)
     ms(A("cr", 0, 256, key=0), float(17 * 2 ** 25))
@@ -252,9 +268,7 @@ def rank_program(g, core, T, topo):
     ms(A("cr", 512, 768, key=2), float(9 * 2 ** 21))
     ms(A("srl"), -2.0)
     ms(A("srx"), -2.0)
-    ms(A("svl"), 0.0)
-    ms(A("svx"), 0.0)
-    ms(A("sz"), 0.0)
+    ms(A("cr", 768, 1024, key=3), 65536.0)
     for i, wgt in enumerate((1.0, 32.0, float(-2 ** 25), float(-2 ** 26))):
         ts(A("gw", 8 * i, 8 * i + 8, key=i), A("gsf"), wgt, Op.mult)
     cp(A("k2b"), A("k2f"))
@@ -262,38 +276,39 @@ def rank_program(g, core, T, topo):
     cp(A("id2", 128, 256, key=1), A("idf"))
     ID2 = (T.id2[:, :], (("id2", 0), ("id2", 1)))
     ONE1 = (T.oneb[0:1, :], (("oneb", None),))
-
-    def constants():
-        ts(A("mkj"), A("mki"), 15, Op.bitwise_and)
-        ts(A("mk"), A("mkj"), 0.0, Op.is_equal)
-        ts(A("rst"), A("k2f"), 0.0, Op.is_equal, 2.0e9, Op.mult)
-        ts(A("rs"), A("rst"), -1.0e9, Op.add)
-        ts(A("rzb"), A("k2f"), 0.0, Op.is_gt)
-        ts(A("rzf"), A("k2f"), 0.0, Op.is_gt)
-        cp(A("pcn", 0, 256, key=0), A("k2f"))
-        ts(A("pcn", 256, 512, key=1), A("k2f"), 65537.0, Op.mult, 16777216.0, Op.add)
-        ts(A("kpi"), A("kpa"), 15, Op.bitwise_and)
-        tt(A("cgp"), A("kpi"), A("ici"), Op.add)
-        ts(A("lmi", 0, 8, key=0), A("limr"), 1, Op.bitwise_and)
-        ts(A("lmi", 8, 16, key=1), A("limr"), 1, Op.arith_shift_right)
-        ts(A("lmi", 16, 24, key=2), A("kpi", 0, 8), 2.0, Op.mult, -16.0, Op.add)
-        cp(A("lmf", 0, 8, key=0), A("lmi", 0, 8, key=0))
-        tt(A("lmf", 8, 16, key=1), A("lmi", 8, 16, key=1), A("lmi", 16, 24, key=2), Op.add)
-        ts(A("lmf", 16, 24, key=2), A("lmf", 8, 16, key=1), float(2 ** 20), Op.mult)
-
-    def first_state():
-        ts(A("fa"), A("lemr"), 32.0, Op.mult)
-        for h in range(2):
-            turn(A("pf", 128 * h, 128 * h + 128, key="l"), A("fa", 128 * h, 128 * h + 128))
-        cp(A("ls", 0, 256, key=0), A("pf", 0, 256, key="l"))
-        ts(A("fb"), A("conr"), 256.0, Op.mult)
-        ts(A("fc"), A("cntr"), 32.0, Op.mult)
-        tt(A("sk"), A("fb"), A("fc"), Op.add)
-        ts(A("fc"), A("orgr"), 2.0, Op.mult)
-        tt(A("fb"), A("sk"), A("fc"), Op.add)
-        for h in range(2):
-            turn(A("px", 128 * h, 128 * h + 128, key="x"), A("fb", 128 * h, 128 * h + 128))
-        cp(A("xs", 0, 256, key=0), A("px", 0, 256, key="x"))
+    ts(A("mkj"), A("mki"), 15, Op.bitwise_and)
+    ts(A("mk"), A("mkj"), 0.0, Op.is_equal)
+    ts(A("rst"), A("k2f"), 0.0, Op.is_equal, 2.0e9, Op.mult)
+    ts(A("rs"), A("rst"), -1.0e9, Op.add)
+    ts(A("rzb"), A("k2f"), 0.0, Op.is_gt)
+    ts(A("rzf"), A("k2f"), 0.0, Op.is_gt)
+    ts(A("lkr"), A("k2f"), 65536.0, Op.mult, 16777216.0, Op.add)
+    tt(A("shm"), A("shf"), A("rzf", 0, 128), Op.mult)
+    tt(A("dmf"), A("shm"), A("idf"), Op.subtract)
+    cp(A("dmb"), A("dmf"))
+    for i, wgt in enumerate((32.0, 256.0)):
+        ts(A("d16", 128 * i, 128 * i + 128, key=i), A("dmf"), wgt, Op.mult)
+    for i, wgt in enumerate((32.0, 256.0, -256.0)):
+        ts(A("i16", 128 * i, 128 * i + 128, key=i), A("idf"), wgt, Op.mult)
+    ts(A("oh"), A("onf", 0, 128), 256.0, Op.mult)
+    ts(A("r16"), A("onf"), 2047.0, Op.mult)
+    ts(A("rk0", 0, 256, key=0), A("k2f"), 0.0, Op.is_equal, -256.0, Op.mult)
+    ts(A("rk0", 256, 512, key=1), A("k2f"), 0.0, Op.is_equal, -2047.0, Op.mult)
+    ts(A("kpi"), A("kpa"), 15, Op.bitwise_and)
+    tt(A("cgp"), A("kpi"), A("ici"), Op.add)
+    ts(A("lmi", 0, 8, key=0), A("limr"), 1, Op.bitwise_and)
+    ts(A("lmi", 8, 16, key=1), A("limr"), 1, Op.arith_shift_right)
+    ts(A("lmi", 16, 24, key=2), A("kpi", 0, 8), 2.0, Op.mult, -16.0, Op.add)
+    cp(A("lmf", 0, 8, key=0), A("lmi", 0, 8, key=0))
+    tt(A("lmf", 8, 16, key=1), A("lmi", 8, 16, key=1), A("lmi", 16, 24, key=2), Op.add)
+    ts(A("lmf", 16, 24, key=2), A("lmf", 8, 16, key=1), float(2 ** 20), Op.mult)
+    for t in range(NV):
+        act(A("lb", 256 * t, 256 * t + 128, key=t), A("oneb"), F.Copy, scale=A("lmf", t, t + 1, key=0))
+        act(A("lb", 256 * t + 128, 256 * t + 256, key=t), A("oneb"), F.Copy, scale=A("lmf", 16 + t, 17 + t, key=2))
+    ts(A("cl", 0, 256, key=0), A("conr"), 16.0, Op.add)
+    ts(A("fb"), A("cntr"), 32.0, Op.mult)
+    ts(A("fc"), A("orgr"), 2.0, Op.mult)
+    tt(A("rl", 0, 256, key=0), A("fb"), A("fc"), Op.add)
 
     def I(j, key=None):
         return A("pi", 16 * j, 16 * j + 16, key=j)
@@ -317,12 +332,45 @@ def rank_program(g, core, T, topo):
     for t in range(NV):
         c0 = 256 * t
         last = t == NV - 1
+        par = t % 2
+        LF, CF, EM = A("lf", 256 * par, 256 * par + 256, key=par), A("cf", 256 * par, 256 * par + 256, key=par), A("em")
+        RF = A("rl", c0, c0 + 256, key=t)
+        half = lambda name, base, key: [A(name, base + 128 * h, base + 128 * h + 128, key=key) for h in range(2)]
+        LFh, CFh, RFh = half("lf", 256 * par, par), half("cf", 256 * par, par), half("rl", c0, t)
+        EMh = half("em", 0, None)
+        ID, IDB = A("idf"), (T.id2[:, 0:128], (("id2", 0),))
+        I32, I256, IM256 = A("i16", 0, 128, key=0), A("i16", 128, 256, key=1), A("i16", 256, 384, key=2)
+        D32, D256, DB = A("d16", 0, 128, key=0), A("d16", 128, 256, key=1), A("dmb")
+        H256 = (T.oh[0:1, :], (("oh", None),))
+        CON, NEW, NAM = A("ia", 0, 16, key=0), A("ia", 16, 32, key=1), A("ia", 32, 48, key=2)
+        B32, CL32, G32 = A("fl", 0, 16, key=0), A("fl", 16, 32, key=1), A("fl", 32, 48, key=2)
+        P3 = [A("p3", 16 * i, 16 * i + 16) for i in range(3)]
         mm(A("pg", 0, 256), ONE1, (T.cr[0:1, 256:512], (("cr", 1),)), True, False)
         mm(A("pk", 0, 256), ONE1, (T.cr[0:1, 512:768], (("cr", 2),)), True, False)
         mm(A("pk", 0, 256), ONE1, (T.k2b[0:1, :], (("k2b", None),)), False, False)
         mm(A("pb", 0, 256), ONE1, (T.cr[0:1, 0:256], (("cr", 0),)), True, False)
         for h in range(2):
-            mm(A("pe", 256 + 8 * h, 264 + 8 * h, key="u"), A("ys", 128 * h, 128 * h + 128), A("gw", 0, 8, key=0), True, True)
+            mm(A("pe", 256 + 8 * h, 264 + 8 * h, key="u"), A("ys", 256 * par + 128 * h, 256 * par + 128 * h + 128, key=par), A("gw", 0, 8, key=0), True, True)
+
+        ts(LF, A("ll", c0, c0 + 256, key=t), -2048.0, Op.add)
+        mm(A("pcn", 0, 256, key="l"), ONE1, (T.lkr[0:1, :], (("lkr", None),)), True, False)
+        mm(A("pcn", 0, 256, key="l"), ONE1, (T.k2b[0:1, :], (("k2b", None),)), False, False)
+        mm(A("pcn", 0, 256, key="l"), ONE1, (T.cr[0:1, 768:1024], (("cr", 3),)), False, False)
+        for h in range(2):
+            mm(A("pcn", 128 * h, 128 * h + 128, key="l"), LFh[h], I32, False, h == 1)
+
+        def sums_l(h):
+            for dst, src, wk in (("pk", "ab", 1), ("pg", "sg", 2)):
+                for k in range(16):
+                    mm(A(dst, 128 * h + k, 128 * h + 128, 16),
+                       (T[src][:, 2048 * h + k:2048 * h + 2048:16], ((src, 2 * h), (src, 2 * h + 1))),
+                       A("gw", 8 * wk, 8 * wk + 8, key=wk), False, h == 1 and k == 15)
+
+        def sums_c(h):
+            for k in range(16):
+                mm(A("pb", 128 * h + k, 128 * h + 128, 16),
+                   (T.cb[:, 2048 * h + k:2048 * h + 2048:16], (("cb", 2 * h), ("cb", 2 * h + 1))),
+                   A("gw", 24, 32, key=3), False, h == 1 and k == 15)
 
         for q in range(4):
             h, lo = q // 2, 1024 * q
@@ -330,60 +378,60 @@ def rank_program(g, core, T, topo):
                A("yr", lo, lo + 1024, key=h), Op.subtract)
             act(A("ab", lo, lo + 1024, key=q), A("dd", lo, lo + 1024, key=q), F.Abs)
             act(A("sg", lo, lo + 1024, key=q), A("dd", lo, lo + 1024, key=q), F.Sign, bias=-0.5)
-            if q % 2 == 1:
-                for k in range(16):
-                    two = (("ab", q - 1), ("ab", q))
-                    mm(A("pk", 128 * h + k, 128 * h + 128, 16), (T.ab[:, 2048 * h + k:2048 * h + 2048:16], two),
-                       A("gw", 8, 16, key=1), False, q == 3 and k == 15)
-                for k in range(16):
-                    two = (("sg", q - 1), ("sg", q))
-                    mm(A("pg", 128 * h + k, 128 * h + 128, 16), (T.sg[:, 2048 * h + k:2048 * h + 2048:16], two),
-                       A("gw", 16, 24, key=2), False, q == 3 and k == 15)
-        if t == 0:
-            ts(A("cl", 0, 256, key=0), A("conr"), 16.0, Op.add)
+            if q == 1:
+                sums_l(0)
+            if q == 2:
+                ts(CF, A("cl", c0, c0 + 256, key=t), -2063.0, Op.add)
+                ts(EM, A("cl", c0, c0 + 256, key=t), 16.0, Op.is_lt, 256.0, Op.mult)
+                mm(A("pcn", 256, 512, key="x"), A("lb", 256 * t, 256 * t + 128, key=t), ID2, True, False)
+                mm(A("pcn", 256, 512, key="x"), A("lb", 256 * t + 128, 256 * t + 256, key=t), ID2, False, False)
+                mm(A("pcn", 256, 512, key="x"), H256, (T.r16[0:1, :], (("r16", None),)), False, False)
+                for h in range(2):
+                    mm(A("pcn", 256 + 128 * h, 384 + 128 * h, key="x"), CFh[h], I256, False, False)
+                for h in range(2):
+                    mm(A("pcn", 256 + 128 * h, 384 + 128 * h, key="x"), RFh[h], IDB, False, h == 1)
+                for h in range(2):
+                    mm(A("pe", 128 * h, 128 * h + 128, key="xs"), RFh[h], IDB, True, False)
+                    mm(A("pe", 128 * h, 128 * h + 128, key="xs"), EMh[h], IDB, False, True)
+        act(A("lk"), A("pcn", 0, 256, key="l"), F.Copy)
+        act(A("xk"), A("pcn", 256, 512, key="x"), F.Copy)
+        op("s", lambda: g.scalar.activation(T.rho[:, :], T.pe[:, 0:256], F.Identity, bias=128.53125, scale=1.0 / 32),
+           [A("rho")], [A("pe", 0, 256, key="xs")])
         for q in range(4):
             h, lo = q // 2, 1024 * q
             w = ind("pt", 0, 4112, "cl", c0 + 64 * q, c0 + 64 * q + 64, t)
             tt(A("cb", lo, lo + 1024, key=q), (w[0], w[1] + (("ptz", None),)), A("yr", lo, lo + 1024, key=h), Op.is_gt)
-            if q % 2 == 1:
-                for k in range(16):
-                    two = (("cb", q - 1), ("cb", q))
-                    mm(A("pb", 128 * h + k, 128 * h + 128, 16), (T.cb[:, 2048 * h + k:2048 * h + 2048:16], two),
-                       A("gw", 24, 32, key=3), False, q == 3 and k == 15)
-        if t == 0:
-            constants()
-            first_state()
-        LS, XS = A("ls", c0, c0 + 256, key=t), A("xs", c0, c0 + 256, key=t)
-        ts(A("dg0"), ID2, A("lmf", t, t + 1, key=0), Op.mult)
-        ts(A("dg1"), ID2, A("lmf", 16 + t, 17 + t, key=2), Op.mult)
-        ALL = A("oneb")
-        mm(A("pe", 0, 256, key="l"), ALL, A("dg0"), True, False)
-        mm(A("pe", 0, 256, key="l"), ALL, A("dg1"), False, True)
-        cp(A("xsi"), XS)
-        ts(A("xsf"), A("xsi"), 0x1000E0, Op.bitwise_and)
-        ts(A("sm"), A("xsf"), 256.0, Op.min, -1.0, Op.mult)
-        tt(A("sk"), A("pcn", 0, 256, key=0), A("sm"), Op.add)
-        scan(A("sm"), A("rs"), A("sk"), 1.0e9, Op.max, Op.min)
-        cp(I(0), A("sm", 15, 256, 16))
-        ts(I(1), I(0), 30, Op.bitwise_and)
+            if q == 1:
+                sums_c(0)
+                sums_l(1)
+        sums_c(1)
         U = L(0)
         cp(U, A("pe", 256, 272, key="u"))
         tt(I(2), U, U, Op.mult)
-        ts(I(3), I(2), 5, Op.arith_shift_right)
         ts(I(4), U, 37.0, Op.mult, float(t), Op.add)
+        ts(I(3), I(2), 5, Op.arith_shift_right)
         tt(I(5), I(3), I(4), Op.add)
-        ts(I(6), I(5), 4095, Op.bitwise_and)
-        tt(A("lk"), A("pcn", 256, 512, key=1), LS, Op.add)
-        tt(A("xk"), A("pe", 0, 256, key="l"), XS, Op.add)
+        ts(NEW, I(5), 4095, Op.bitwise_and)
+        ts(A("smb"), A("rho"), 137.0, Op.min, -32.0, Op.mult)
+        mm((T.ph[:, :], (("ph", "l"), ("ph", "x"))), H256, (T.rk0[0:1, :], (("rk0", 0), ("rk0", 1))), True, False)
+        for h in range(2):
+            mm(A("ph", 128 * h, 128 * h + 128, key="l"), LFh[h], D32, False, False)
+        for h in range(2):
+            mm(A("ph", 256 + 128 * h, 384 + 128 * h, key="x"), CFh[h], D256, False, False)
+        for h in range(2):
+            mm(A("ph", 256 + 128 * h, 384 + 128 * h, key="x"), RFh[h], DB, False, h == 1)
+        mm(A("pf", 0, 256), I32, LF, True, False)
+        mm(A("px", 256, 512, key="s"), ONE1, (T.k2b[0:1, :], (("k2b", None),)), True, False)
+        mm(A("px", 256, 512, key="s"), IDB, A("smb"), False, True)
         tt(A("kg"), A("pg", 0, 256), A("lk"), Op.max)
         tt(A("qq"), A("pk", 0, 256), A("kg"), Op.min)
-        tt(A("ph", 0, 256, key=0), A("pb", 0, 256), A("xk"), Op.max)
-        tt(A("key"), A("ph", 0, 256, key=0), A("qq"), Op.min)
+        tt(A("pk", 256, 512, key="b"), A("pb", 0, 256), A("xk"), Op.max)
+        tt(A("key"), A("pk", 256, 512, key="b"), A("qq"), Op.min)
         scan(A("pm"), A("rs"), A("key"), 1.0e9, Op.max, Op.min)
         M = I(7)
         cp(M, A("pm", 15, 256, 16))
         a, j = I(8), I(9)
-        B32, CL32, NB32, G32 = L(1), L(2), L(3), L(4)
+        NB32 = L(3)
         ts(a, M, 5, Op.arith_shift_right, 4095, Op.bitwise_and)
         ts(NB32, M, 16777216.0, Op.is_ge, 32.0, Op.mult)
         ts(CL32, M, 16777216.0 + 2097152.0, Op.is_ge, 32.0, Op.mult)
@@ -399,76 +447,63 @@ def rank_program(g, core, T, topo):
         ts(I(19), M, 30, Op.bitwise_and)
         ts(j, I(13), 3840, Op.bitwise_and)
         tt(L(5), I(15), I(16), Op.add)
-        ts(I(18), M, 8, Op.arith_shift_right, 4095, Op.bitwise_and)
-        tt(I(17), j, A("cc"), Op.add)
+        ts(CON, M, 8, Op.arith_shift_right, 4095, Op.bitwise_and)
+        tt(NAM, j, A("cc"), Op.add)
+        s3 = L(5)
         if t:
-            for h in range(2):
-                ts((T.pl[:, 96 + 8 * h:104 + 8 * h], (("pl", 6),)), (T.pl[:, 80 + 8 * h:88 + 8 * h], (("pl", 5),)),
-                   A("wf", h, h + 1), Op.add)
+            tt(L(6), L(5), A("w8"), Op.add)
             s3 = L(6)
-        else:
-            s3 = L(5)
-        tt(L(8), I(18), B32, Op.mult)
-        tt(L(9), I(6), CL32, Op.mult)
+        tt(A("p3"), (T.ia[:, :], CON[1] + NEW[1] + NAM[1]), (T.fl[:, :], B32[1] + CL32[1] + G32[1]), Op.mult)
         tt(L(7), I(14), s3, Op.is_lt)
-        tt(L(10), I(17), G32, Op.mult)
-        tt(L(11), L(8), L(9), Op.add)
+        tt(L(11), P3[0], P3[1], Op.add)
         tt(L(12), L(7), B32, Op.mult)
-        tt(A("svl", 0, 256, 16), L(11), L(10), Op.add)
+        tt(L(13), L(11), P3[2], Op.add)
         tt(A("srl", 0, 256, 16), L(12), I(19), Op.add)
-        scan(A("ph", 0, 256, key=0), A("rzf"), A("svl"), 0.0, Op.mult, Op.add)
+        DL = A("ph", 0, 256, 16, key="l")
+        tt(DL, DL, L(13), Op.add)
         scan(A("ra"), A("rzb"), A("srl"), 0.0, Op.mult, Op.add)
-        tt(A("ph", 256, 512, key=1), A("ph", 0, 256, key=0), LS, Op.subtract)
+        scan(A("pk", 0, 256), A("rzf"), A("ph", 0, 256, key="l"), 0.0, Op.mult, Op.add)
         ts(A("ma"), A("ra"), 0.0, Op.is_equal)
-        LO = A("lso", c0, c0 + 256, key=t)
-        tt(A("ph", 0, 256, key=0), A("ph", 256, 512, key=1), A("ma"), Op.mult)
-        ts(I(20), M, 21, Op.arith_shift_right)
-        ts(I(23), M, 0xFFFE0, Op.bitwise_and)
-        tt(LO, A("ph", 0, 256, key=0), LS, Op.add)
-        for h in range(2):
-            turn(A("pf", 128 * h, 128 * h + 128, key="l"), A("lso", c0 + 128 * h, c0 + 128 * h + 128, key=t))
-        ts(L(14), I(20), 2.0, Op.mult, 16.0, Op.add)
-        ts(L(15), M, 16777216.0, Op.is_lt)
-        tt(L(16), L(14), I(1), Op.subtract)
-        ts(L(20), I(23), 1.0 / 32, Op.mult, 1.0, Op.add)
-        tt(L(17), L(16), L(15), Op.mult)
-        tt(L(21), L(20), L(12), Op.mult)
-        tt(L(18), L(17), I(1), Op.add)
-        tt(L(22), B32, L(12), Op.subtract)
         tt(L(23), a, G32, Op.mult)
-        tt(A("srx", 0, 256, 16), L(18), CL32, Op.add)
-        tt(L(24), L(23), L(22), Op.subtract)
-        tt(L(26), L(21), I(19), Op.add)
-        ts(L(25), L(24), 8.0, Op.mult)
-        if not last:
-            ts(A("llo", c0, c0 + 256, key=t), A("pf", 0, 256, key="l"), 1.0 / 32, Op.mult)
-            send("llo", "ll", "al", t)
-        tt(A("svx", 0, 256, 16), L(25), L(26), Op.add)
-        scan(A("rb"), A("rzb"), A("srx"), 0.0, Op.mult, Op.add)
-        scan(A("ph", 0, 256, key=0), A("rzf"), A("svx"), 0.0, Op.mult, Op.add)
-        ts(A("mb"), A("rb"), 0.0, Op.is_equal)
-        tt(A("ph", 256, 512, key=1), A("ph", 0, 256, key=0), XS, Op.subtract)
-        ts(L(28), j, -4096.0, Op.add, 1.0 / 8192, Op.mult)
-        tt(A("ph", 0, 256, key=0), A("ph", 256, 512, key=1), A("mb"), Op.mult)
-        tt(L(29), L(23), G32, Op.add)
-        tt(A("xso", c0, c0 + 256, key=t), A("ph", 0, 256, key=0), XS, Op.add)
+        tt(A("dml"), A("pk", 0, 256), A("ma"), Op.mult)
         for h in range(2):
-            turn(A("px", 128 * h, 128 * h + 128, key="x"), A("xso", c0 + 128 * h, c0 + 128 * h + 128, key=t))
+            mm(A("pf", 128 * h, 128 * h + 128), A("dml", 128 * h, 128 * h + 128), ID, False, h == 1)
+        ts(L(28), j, -4096.0, Op.add, 1.0 / 8192, Op.mult)
+        tt(L(29), L(23), G32, Op.add)
         tt(L(30), L(28), G32, Op.mult)
-        tt(A("sz", 0, 256, 16), L(30), L(29), Op.add)
-        scan(A("ph", 0, 256, key=0), A("rzf"), A("sz"), 0.0, Op.mult, Op.add)
-        tt(A("zx"), A("ph", 0, 256, key=0), A("mk"), Op.mult)
+        ts(I(20), M, 21, Op.arith_shift_right)
+        tt(A("zz"), L(30), L(29), Op.add)
+        for i in range(16):
+            act(A("zx", 16 * i, 16 * i + 16), A("mk"), F.Copy, scale=(T.zz[:, i:i + 1], (("zz", None),)))
         for h in range(2):
             mm(A("pe", 272 + 8 * h, 280 + 8 * h, key="z"), A("zx", 128 * h, 128 * h + 128), A("gsf"), True, True)
         if not last:
-            ts(A("clo", c0, c0 + 256, key=t), A("px", 0, 256, key="x"), 1.0 / 256, Op.mult, 15.502, Op.add)
-            send("clo", "cl", "ac", t)
-            send("xso", "xs", "ax", t)
-            send("lso", "ls", "as", t)
             for h in range(2):
-                op("s", lambda: g.scalar.activation(T.wj[:, 8 * h:8 * h + 8], T.pl[:, 16 + 8 * h:24 + 8 * h], F.Copy,
+                op("s", lambda: g.scalar.activation(T.wj[:, 8 * h:8 * h + 8], T.fl[:, 8 * h:8 * h + 8], F.Copy,
                                                     accum_out=T.ws[:, h:h + 1]),
                    [A("wj", key=h), A("ws", key=h)], [B32])
+        scan(A("sm"), A("rs"), A("px", 256, 512, key="s"), 1.0e9, Op.max, Op.min)
+        mm(A("px", 0, 256), I256, CF, True, False)
+        mm(A("px", 0, 256), IDB, RF, False, False)
+        ts(I(23), M, 0xFFFE0, Op.bitwise_and)
+        ts(L(14), I(20), 2.0, Op.mult, 16.0, Op.add)
+        cp(I(0), A("sm", 15, 256, 16))
+        ts(L(15), M, 16777216.0, Op.is_lt)
+        ts(L(20), I(23), 1.0 / 32, Op.mult, 1.0, Op.add)
+        ts(I(1), I(0), 30, Op.bitwise_and)
+        tt(L(22), B32, L(12), Op.subtract)
+        tt(L(21), L(20), L(12), Op.mult)
+        tt(L(16), L(14), I(1), Op.subtract)
+        tt(L(24), L(23), L(22), Op.subtract)
+        tt(L(26), L(21), I(19), Op.add)
+        tt(L(17), L(16), L(15), Op.mult)
+        ts(L(25), L(24), 8.0, Op.mult)
+        if not last:
+            ts(A("llo", c0, c0 + 256, key=t), A("pf", 0, 256), 1.0 / 32, Op.mult, 2048.0, Op.add)
+            send("llo", "ll", "al", t)
+        tt(L(18), L(17), I(1), Op.add)
+        tt(L(27), L(25), L(26), Op.add)
+        tt(A("srx", 0, 256, 16), L(18), CL32, Op.add)
         ts(I(24), A("pe", 272, 288, key="z"), 16.0, Op.add)
         ts(I(25), I(24), 5, Op.arith_shift_right)
         ts(I(26), I(24), 31, Op.bitwise_and)
@@ -476,27 +511,47 @@ def rank_program(g, core, T, topo):
         ts(I(27), I(26), 256.0, Op.mult)
         w = ind("pt", 0, 4112, "aof", 0, 16, None)
         w = (w[0], w[1] + (("ptz", None),))
-        Y = A("ys")
+        Y = A("ys", 256 * par, 256 * par + 256, key=par)
         tt(A("ee"), w, Y, Op.subtract)
-        tt(I(28), I(27), A("cgp"), Op.add)
-        tt(A("mn"), w, Y, Op.min)
-        cp(A("nof"), I(28))
-        act(Y, A("ee"), F.Abs)
-        op("v", lambda: g.vector.tensor_copy(T.pt[:, 16:PW].indirect(T.nof[:, 0:16]), T.mn[:, :]),
-           [A("pt")], [A("mn"), A("nof")])
+        act(A("ys", 256 - 256 * par, 512 - 256 * par, key=1 - par), A("ee"), F.Abs)
         if not last:
-            spread(0)
-            spread(1)
-            cpw = (T.ws[:, 0:2], (("ws", 0), ("ws", 1)))
-            ts(A("wi", 0, 2), cpw, 1.0 / 32, Op.mult)
+            spread(0, 1 - par)
+        DX = A("ph", 256, 512, 16, key="x")
+        tt(DX, DX, L(27), Op.add)
+        scan(A("rb"), A("rzb"), A("srx"), 0.0, Op.mult, Op.add)
+        scan(A("pk", 0, 256), A("rzf"), A("ph", 256, 512, key="x"), 0.0, Op.mult, Op.add)
+        ts(A("mb"), A("rb"), 0.0, Op.is_equal)
+        tt(I(28), I(27), A("cgp"), Op.add)
+        tt(A("dmx"), A("pk", 0, 256), A("mb"), Op.mult)
+        for h in range(2):
+            mm(A("px", 128 * h, 128 * h + 128), A("dmx", 128 * h, 128 * h + 128), ID, False, h == 1)
+        ts(A("mn"), A("ee"), 0.0, Op.min)
+        cp(A("nof"), I(28))
+        op("v", lambda: g.vector.tensor_tensor(T.pt[:, 16:PW].indirect(T.nof[:, 0:16]), A("mn")[0], Y[0], Op.add),
+           [A("pt")], [A("mn"), Y, A("nof")])
+        if not last:
+            ts(A("clo", c0, c0 + 256, key=t), A("px", 0, 256), 1.0 / 256, Op.mult, 2062.502, Op.add)
+            send("clo", "cl", "ac", t)
+            act(A("xn"), A("px", 0, 256), F.Copy)
+            spread(1, 1 - par)
+            ts(A("wi", 0, 2), (T.ws[:, 0:2], (("ws", 0), ("ws", 1))), 1.0 / 32, Op.mult)
             ts(A("wk", 0, 2), A("wi", 0, 2), 3, Op.bitwise_and)
             cp(A("wf", 0, 2), A("wk", 0, 2))
+            CN = A("cf", 256 - 256 * par, 512 - 256 * par, key=1 - par)
+            ts(CN, A("clo", c0, c0 + 256, key=t), -2063.0, Op.add)
+            mm(A("pf", 256, 512, key="r"), ID, A("xn"), True, False)
+            mm(A("pf", 256, 512, key="r"), IM256, CN, False, True)
+            act(A("rlo", c0, c0 + 256, key=t), A("pf", 256, 512, key="r"), F.Copy)
+            send("rlo", "rl", "ar", t)
+            for h in range(2):
+                op("s", lambda: g.scalar.activation(T.w8[:, 8 * h:8 * h + 8], T.onf[:, 0:8], F.Copy, scale=T.wf[:, h:h + 1]),
+                   [A("w8")], [A("onf"), A("wf", 0, 2)], selfok=True)
 
     dma("y", T.zp[:, :], T.pt[:, 16:4112], "o0", [("zp", None)], [("pt", None)])
-    dma("s", T.zy[:, :], T.ys[:, :], "o1", [("zy", None)], [("ys", None)])
-    ts(A("ofl"), A("pf", 0, 256, key="l"), 1.0 / 32, Op.mult)
+    dma("s", T.zy[:, :], T.ys[:, 0:256], "o1", [("zy", None)], [("ys", 0)])
+    ts(A("ofl"), A("pf", 0, 256), 1.0 / 32, Op.mult, 2048.0, Op.add)
     dma("y", T.zl[:, :], T.ofl[:, :], "o2", [("zl", None)], [("ofl", None)])
-    cp(A("xsi"), A("px", 0, 256, key="x"))
+    ts(A("xsi"), A("px", 0, 256), 524032.0, Op.add)
     ts(A("oi", 0, 256, key=0), A("xsi"), 8, Op.arith_shift_right)
     ts(A("oi", 256, 512, key=1), A("xsi"), 1, Op.arith_shift_right, 15, Op.bitwise_and)
     ts(A("oi", 512, 768, key=2), A("xsi"), 5, Op.arith_shift_right, 7, Op.bitwise_and)

from concourse.mybir import dt, AluOpType, AxisListType, ActivationFunctionType
import comms_topo

NV = 8
PW = 16 + 4096 + 256

SCRATCH = {
    "pt": ("sbuf", [128, PW], "bfloat16"),
    "ys": ("sbuf", [128, 512], "bfloat16"),
    "yr": ("sbuf", [128, 4096], "bfloat16"),
    "dd": ("sbuf", [128, 4096], "bfloat16"),
    "ab": ("sbuf", [128, 4096], "bfloat16"),
    "sg": ("sbuf", [128, 4096], "bfloat16"),
    "cb": ("sbuf", [128, 4096], "bfloat16"),
    "lemr": ("sbuf", [128, 256], "int32"),
    "conr": ("sbuf", [128, 256], "int32"),
    "orgr": ("sbuf", [128, 256], "bfloat16"),
    "cntr": ("sbuf", [128, 256], "bfloat16"),
    "limr": ("sbuf", [128, 8], "int32"),
    "ll": ("sbuf", [128, 256 * NV], "uint16"),
    "cl": ("sbuf", [128, 256 * NV], "uint16"),
    "rl": ("sbuf", [128, 256 * NV], "bfloat16"),
    "llo": ("sbuf", [128, 256 * NV], "uint16"),
    "clo": ("sbuf", [128, 256 * NV], "uint16"),
    "rlo": ("sbuf", [128, 256 * NV], "bfloat16"),
    "onf": ("sbuf", [128, 256], "float32"),
    "idf": ("sbuf", [128, 128], "float32"),
    "id2": ("sbuf", [128, 256], "bfloat16"),
    "gsf": ("sbuf", [128, 8], "float32"),
    "gst": ("sbuf", [128, 8], "float32"),
    "gw": ("sbuf", [128, 32], "bfloat16"),
    "k2f": ("sbuf", [128, 256], "float32"),
    "k2b": ("sbuf", [128, 256], "bfloat16"),
    "oneb": ("sbuf", [128, 128], "bfloat16"),
    "cr": ("sbuf", [128, 1024], "bfloat16"),
    "mki": ("sbuf", [128, 16], "int32"),
    "mkj": ("sbuf", [128, 16], "int32"),
    "mk": ("sbuf", [128, 16], "float32"),
    "rs": ("sbuf", [128, 256], "float32"),
    "rst": ("sbuf", [128, 256], "float32"),
    "rzb": ("sbuf", [128, 256], "bfloat16"),
    "rzf": ("sbuf", [128, 256], "float32"),
    "srl": ("sbuf", [128, 256], "bfloat16"),
    "srx": ("sbuf", [128, 256], "bfloat16"),
    "lb": ("sbuf", [128, 2048], "bfloat16"),
    "lkr": ("sbuf", [128, 256], "bfloat16"),
    "lf": ("sbuf", [128, 512], "float16"),
    "cf": ("sbuf", [128, 512], "float16"),
    "em": ("sbuf", [128, 256], "bfloat16"),
    "rho": ("sbuf", [128, 256], "bfloat16"),
    "dmb": ("sbuf", [128, 128], "bfloat16"),
    "d16": ("sbuf", [128, 256], "float16"),
    "i16": ("sbuf", [128, 384], "float16"),
    "oh": ("sbuf", [128, 128], "float16"),
    "r16": ("sbuf", [128, 256], "float16"),
    "rk0": ("sbuf", [128, 512], "float16"),
    "xn": ("sbuf", [128, 256], "float32"),
    "shf": ("sbuf", [128, 128], "float32"),
    "shm": ("sbuf", [128, 128], "float32"),
    "dmf": ("sbuf", [128, 128], "float32"),
    "dml": ("sbuf", [128, 256], "float32"),
    "dmx": ("sbuf", [128, 256], "float32"),
    "ia": ("sbuf", [128, 48], "int32"),
    "fl": ("sbuf", [128, 48], "float32"),
    "p3": ("sbuf", [128, 48], "float32"),
    "zz": ("sbuf", [128, 16], "float32"),
    "smb": ("sbuf", [128, 256], "bfloat16"),
    "w8": ("sbuf", [128, 16], "float32"),
    "kpi": ("sbuf", [128, 16], "int32"),
    "kpa": ("sbuf", [128, 16], "int32"),
    "ici": ("sbuf", [128, 16], "int32"),
    "cgp": ("sbuf", [128, 16], "int32"),
    "cc": ("sbuf", [128, 16], "int32"),
    "lmi": ("sbuf", [128, 32], "int32"),
    "lmf": ("sbuf", [128, 24], "float32"),
    "fb": ("sbuf", [128, 256], "float32"),
    "fc": ("sbuf", [128, 256], "float32"),
    "xsi": ("sbuf", [128, 256], "int32"),
    "xsf": ("sbuf", [128, 256], "int32"),
    "sk": ("sbuf", [128, 256], "float32"),
    "sm": ("sbuf", [128, 256], "float32"),
    "xk": ("sbuf", [128, 256], "float32"),
    "lk": ("sbuf", [128, 256], "float32"),
    "kg": ("sbuf", [128, 256], "float32"),
    "qq": ("sbuf", [128, 256], "float32"),
    "key": ("sbuf", [128, 256], "float32"),
    "pm": ("sbuf", [128, 256], "float32"),
    "ra": ("sbuf", [128, 256], "bfloat16"),
    "ma": ("sbuf", [128, 256], "bfloat16"),
    "rb": ("sbuf", [128, 256], "bfloat16"),
    "mb": ("sbuf", [128, 256], "bfloat16"),
    "zx": ("sbuf", [128, 256], "float32"),
    "pi": ("sbuf", [128, 16 * 40], "int32"),
    "pl": ("sbuf", [128, 16 * 40], "float32"),
    "wj": ("sbuf", [128, 16], "float32"),
    "ws": ("sbuf", [128, 16], "float32"),
    "wi": ("sbuf", [128, 16], "int32"),
    "wk": ("sbuf", [128, 16], "int32"),
    "wf": ("sbuf", [128, 16], "float32"),
    "aof": ("sbuf", [128, 16], "uint16"),
    "nof": ("sbuf", [128, 16], "uint16"),
    "ee": ("sbuf", [128, 256], "bfloat16"),
    "mn": ("sbuf", [128, 256], "bfloat16"),
    "ofl": ("sbuf", [128, 256], "float32"),
    "ofc": ("sbuf", [128, 256], "float32"),
    "obo": ("sbuf", [128, 256], "bfloat16"),
    "obb": ("sbuf", [128, 256], "bfloat16"),
    "oi": ("sbuf", [128, 768], "int32"),
    "pb": ("psum", [128, 512], "float32"),
    "pg": ("psum", [128, 512], "float32"),
    "pk": ("psum", [128, 512], "float32"),
    "pcn": ("psum", [128, 512], "float32"),
    "pe": ("psum", [128, 512], "float32"),
    "pf": ("psum", [128, 512], "float32"),
    "px": ("psum", [128, 512], "float32"),
    "ph": ("psum", [128, 512], "float32"),
}
PSUM = ("pb", "pg", "pk", "pcn", "pe", "pf", "px", "ph")
SEMAPHORES = (["sv", "ss", "st", "sp", "loc"] + ["i%d" % i for i in range(7)] + ["o%d" % i for i in range(6)]
              + ["%s%d" % (a, t) for a in ("al", "ac", "ar") for t in range(1, NV)])


def rank_program(g, core, T, topo):
    rank = T.rank_of(core)
    if rank is None:
        return
    n = len(T.cores)
    nxt, prv = T.cores[(rank + 1) % n], T.cores[(rank - 1) % n]
    Op = AluOpType
    F = ActivationFunctionType
    queue = {"v": g.vector, "s": g.scalar, "t": g.tensor, "p": g, "y": g.sync}
    own = {"v": "sv", "s": "ss", "t": "st", "p": "sp"}
    count = {"v": 0, "s": 0, "t": 0, "p": 0}
    known = {q: {} for q in queue}
    wrote, readers, touched = {}, {}, {}

    def A(name, lo=None, hi=None, step=None, key=None):
        t = T[name]
        ap = t[:, :] if lo is None else (t[:, lo:hi] if step is None else t[:, lo:hi:step])
        return (ap, ((name, key),))

    def need(q, reads, writes, selfok):
        want = {}

        def add(tok, free=False):
            if free and tok[0] == own.get(q):
                return
            if want.get(tok[0], 0) < tok[1]:
                want[tok[0]] = tok[1]
        for k in reads:
            for tok in wrote.get(k, ()):
                add(tok)
        for k in writes:
            for tok in wrote.get(k, ()):
                add(tok, selfok)
            for tok in readers.get(k, {}).items():
                add(tok, selfok)
        for k in list(reads) + list(writes):
            if k[0] in PSUM:
                for e, tok in touched.get(k[0], {}).items():
                    if e != q:
                        add(tok)
        for s, v in want.items():
            if known[q].get(s, 0) < v:
                queue[q].wait_ge(T.sem[s], v)
                known[q][s] = v

    def note(q, tok, reads, writes):
        for k in writes:
            wrote[k] = [tok]
            readers[k] = {}
        for k in reads:
            r = readers.setdefault(k, {})
            r[tok[0]] = max(r.get(tok[0], 0), tok[1])
        for k in list(reads) + list(writes):
            if k[0] in PSUM:
                touched.setdefault(k[0], {})[q] = tok

    def op(q, call, outs, ins, selfok=False):
        reads = [k for o in ins for k in o[1]]
        writes = [k for o in outs for k in o[1]]
        need(q, reads, writes, selfok)
        count[q] += 1
        call().then_inc(T.sem[own[q]], 1)
        note(q, (own[q], count[q]), reads, writes)

    def tt(o, a, b, f):
        op("v", lambda: g.vector.tensor_tensor(o[0], a[0], b[0], f), [o], [a, b])

    def ts(o, a, s1, f1, s2=None, f2=None):
        col = [s1] if isinstance(s1, tuple) else []
        x = s1[0] if col else s1
        if f2 is None:
            op("v", lambda: g.vector.tensor_scalar(o[0], a[0], x, None, f1), [o], [a] + col)
        else:
            op("v", lambda: g.vector.tensor_scalar(o[0], a[0], x, s2, f1, f2), [o], [a] + col)

    def cp(o, a):
        op("v", lambda: g.vector.tensor_copy(o[0], a[0]), [o], [a])

    def ms(o, c):
        op("v", lambda: g.vector.memset(o[0], c), [o], [])

    def scan(o, d0, d1, init, f0, f1):
        op("v", lambda: g.vector.tensor_tensor_scan(o[0], d0[0], d1[0], init, f0, f1), [o], [d0, d1])

    def act(o, a, f, bias=0.0, acc=None, scale=None):
        if scale is not None:
            op("s", lambda: g.scalar.activation(o[0], a[0], f, scale=scale[0]), [o], [a, scale], selfok=True)
        elif acc is None:
            op("s", lambda: g.scalar.activation(o[0], a[0], f, bias=bias), [o], [a])
        else:
            op("s", lambda: g.scalar.activation(o[0], a[0], f, accum_out=acc[0]), [o, acc], [a])

    def mm(o, l, r, start, stop):
        op("t", lambda: g.tensor.matmul(o[0], l[0], r[0], start, stop), [o], [l, r], selfok=True)

    def dma(q, o, a, sem, okeys, ikeys):
        need(q, ikeys, okeys, False)
        queue[q].dma_start(o, a).then_inc(T.sem[sem], 16)
        note(q, (sem, 16), ikeys, okeys)

    def ind(name, lo, hi, off, olo, ohi, okey):
        return (T[name][:, lo:hi].indirect(T[off][:, olo:ohi]), ((name, None), (off, okey)))

    dma("y", T.lemr[:, :], T.lem[:, :], "i0", [("lemr", None)], [])
    dma("s", T.ys[:, 0:256], T.ex[:, :], "i1", [("ys", 0)], [])
    dma("s", T.pt[:, 16:4112], T.prop[:, :], "i2", [("pt", None)], [])
    dma("y", T.conr[:, :], T.con[:, :], "i3", [("conr", None)], [])
    dma("y", T.cntr[:, :], T.cnt[:, :], "i4", [("cntr", None)], [])
    dma("y", T.orgr[:, :], T.org[:, :], "i5", [("orgr", None)], [])
    dma("y", T.limr[:, :], T.lim[:, :], "i6", [("limr", None)], [])

    op("v", lambda: g.vector.memset(T.pt[:, 0:16], 0.0), [(None, (("ptz", None),))], [])
    ms(A("onf"), 1.0)

    def p_iota(o, pattern, base, cm, flag):
        if flag:
            op("p", lambda: g.iota(o[0], pattern, base, cm, allow_small_or_imprecise_dtypes=True), [o], [])
        else:
            op("p", lambda: g.iota(o[0], pattern, base, cm), [o], [])

    def p_sel(o, a, pattern, f, base, cm):
        op("p", lambda: g.affine_select(o[0], a[0], pattern, f, 0.0, base, cm), [o], [a])
    p_iota(A("k2f"), [[0, 16], [2, 16]], 0, 0, True)
    p_sel(A("gst"), A("onf", 0, 8), [[-16, 8]], Op.is_ge, 0, 1)
    p_sel(A("gsf"), A("gst"), [[16, 8]], Op.is_ge, 15, -1)
    p_sel(A("idf"), A("onf", 0, 128), [[-1, 128]], Op.is_equal, 0, 1)
    p_iota(A("kpa"), [[0, 16]], 0, 1, False)
    p_iota(A("ici"), [[16, 16]], 0, 0, False)
    p_iota(A("cc"), [[128, 2], [0, 8]], 0, 1, False)
    p_iota(A("mki"), [[-1, 16]], 0, 1, False)
    p_sel(A("shf"), A("onf", 0, 128), [[-1, 128]], Op.is_equal, 1, 1)

    cp(A("ll", 0, 256, key=0), A("lemr"))

    def spread(h, par):
        for k in range(16):
            o = A("yr", 2048 * h + k, 2048 * h + 2048, 16, key=h)
            a = A("ys", 256 * par + 128 * h, 256 * par + 128 * h + 128, key=par)
            op("s", lambda: g.scalar.activation(o[0], a[0], F.Copy), [o], [a], selfok=True)
    spread(0, 0)
    spread(1, 0)

    ms(A("oneb"), 1.0)
    ms(A("cr", 0, 256, key=0), float(17 * 2 ** 25))
    ms(A("cr", 256, 512, key=1), float(2 ** 25))
    ms(A("cr", 512, 768, key=2), float(9 * 2 ** 21))
    ms(A("srl"), -2.0)
    ms(A("srx"), -2.0)
    ms(A("cr", 768, 1024, key=3), 65536.0)
    for i, wgt in enumerate((1.0, 32.0, float(-2 ** 25), float(-2 ** 26))):
        ts(A("gw", 8 * i, 8 * i + 8, key=i), A("gsf"), wgt, Op.mult)
    cp(A("k2b"), A("k2f"))
    cp(A("id2", 0, 128, key=0), A("idf"))
    cp(A("id2", 128, 256, key=1), A("idf"))
    ID2 = (T.id2[:, :], (("id2", 0), ("id2", 1)))
    ONE1 = (T.oneb[0:1, :], (("oneb", None),))
    ts(A("mkj"), A("mki"), 15, Op.bitwise_and)
    ts(A("mk"), A("mkj"), 0.0, Op.is_equal)
    ts(A("rst"), A("k2f"), 0.0, Op.is_equal, 2.0e9, Op.mult)
    ts(A("rs"), A("rst"), -1.0e9, Op.add)
    ts(A("rzb"), A("k2f"), 0.0, Op.is_gt)
    ts(A("rzf"), A("k2f"), 0.0, Op.is_gt)
    ts(A("lkr"), A("k2f"), 65536.0, Op.mult, 16777216.0, Op.add)
    tt(A("shm"), A("shf"), A("rzf", 0, 128), Op.mult)
    tt(A("dmf"), A("shm"), A("idf"), Op.subtract)
    cp(A("dmb"), A("dmf"))
    for i, wgt in enumerate((32.0, 256.0)):
        ts(A("d16", 128 * i, 128 * i + 128, key=i), A("dmf"), wgt, Op.mult)
    for i, wgt in enumerate((32.0, 256.0, -256.0)):
        ts(A("i16", 128 * i, 128 * i + 128, key=i), A("idf"), wgt, Op.mult)
    ts(A("oh"), A("onf", 0, 128), 256.0, Op.mult)
    ts(A("r16"), A("onf"), 2047.0, Op.mult)
    ts(A("rk0", 0, 256, key=0), A("k2f"), 0.0, Op.is_equal, -256.0, Op.mult)
    ts(A("rk0", 256, 512, key=1), A("k2f"), 0.0, Op.is_equal, -2047.0, Op.mult)
    ts(A("kpi"), A("kpa"), 15, Op.bitwise_and)
    tt(A("cgp"), A("kpi"), A("ici"), Op.add)
    ts(A("lmi", 0, 8, key=0), A("limr"), 1, Op.bitwise_and)
    ts(A("lmi", 8, 16, key=1), A("limr"), 1, Op.arith_shift_right)
    ts(A("lmi", 16, 24, key=2), A("kpi", 0, 8), 2.0, Op.mult, -16.0, Op.add)
    cp(A("lmf", 0, 8, key=0), A("lmi", 0, 8, key=0))
    tt(A("lmf", 8, 16, key=1), A("lmi", 8, 16, key=1), A("lmi", 16, 24, key=2), Op.add)
    ts(A("lmf", 16, 24, key=2), A("lmf", 8, 16, key=1), float(2 ** 20), Op.mult)
    for t in range(NV):
        act(A("lb", 256 * t, 256 * t + 128, key=t), A("oneb"), F.Copy, scale=A("lmf", t, t + 1, key=0))
        act(A("lb", 256 * t + 128, 256 * t + 256, key=t), A("oneb"), F.Copy, scale=A("lmf", 16 + t, 17 + t, key=2))
    ts(A("cl", 0, 256, key=0), A("conr"), 16.0, Op.add)
    ts(A("fb"), A("cntr"), 32.0, Op.mult)
    ts(A("fc"), A("orgr"), 2.0, Op.mult)
    tt(A("rl", 0, 256, key=0), A("fb"), A("fc"), Op.add)

    def I(j, key=None):
        return A("pi", 16 * j, 16 * j + 16, key=j)

    def L(j):
        return A("pl", 16 * j, 16 * j + 16, key=j)

    rid, pid, _ = topo.addr(nxt)
    mask = topo.mask(core, nxt)
    n_in = len(topo.engines(prv, core))
    n_out = len(topo.engines(core, nxt))
    sent = [0]

    def send(src, dst, sem, t):
        need("p", [(src, t)], [], False)
        g.remote_dma(T[dst][:, 256 * (t + 1):256 * (t + 2)], T[src][:, 256 * t:256 * (t + 1)],
                     T.sem["%s%d" % (sem, t + 1)], T.sem.loc, pid, rid, mask)
        sent[0] += n_out
        wrote[(dst, t + 1)] = [("%s%d" % (sem, t + 1), n_in)]

    for t in range(NV):
        c0 = 256 * t
        last = t == NV - 1
        par = t % 2
        LF, CF, EM = A("lf", 256 * par, 256 * par + 256, key=par), A("cf", 256 * par, 256 * par + 256, key=par), A("em")
        RF = A("rl", c0, c0 + 256, key=t)
        half = lambda name, base, key: [A(name, base + 128 * h, base + 128 * h + 128, key=key) for h in range(2)]
        LFh, CFh, RFh = half("lf", 256 * par, par), half("cf", 256 * par, par), half("rl", c0, t)
        EMh = half("em", 0, None)
        ID, IDB = A("idf"), (T.id2[:, 0:128], (("id2", 0),))
        I32, I256, IM256 = A("i16", 0, 128, key=0), A("i16", 128, 256, key=1), A("i16", 256, 384, key=2)
        D32, D256, DB = A("d16", 0, 128, key=0), A("d16", 128, 256, key=1), A("dmb")
        H256 = (T.oh[0:1, :], (("oh", None),))
        CON, NEW, NAM = A("ia", 0, 16, key=0), A("ia", 16, 32, key=1), A("ia", 32, 48, key=2)
        B32, CL32, G32 = A("fl", 0, 16, key=0), A("fl", 16, 32, key=1), A("fl", 32, 48, key=2)
        P3 = [A("p3", 16 * i, 16 * i + 16) for i in range(3)]
        mm(A("pg", 0, 256), ONE1, (T.cr[0:1, 256:512], (("cr", 1),)), True, False)
        mm(A("pk", 0, 256), ONE1, (T.cr[0:1, 512:768], (("cr", 2),)), True, False)
        mm(A("pk", 0, 256), ONE1, (T.k2b[0:1, :], (("k2b", None),)), False, False)
        mm(A("pb", 0, 256), ONE1, (T.cr[0:1, 0:256], (("cr", 0),)), True, False)
        for h in range(2):
            mm(A("pe", 256 + 8 * h, 264 + 8 * h, key="u"), A("ys", 256 * par + 128 * h, 256 * par + 128 * h + 128, key=par), A("gw", 0, 8, key=0), True, True)

        ts(LF, A("ll", c0, c0 + 256, key=t), -2048.0, Op.add)
        mm(A("pcn", 0, 256, key="l"), ONE1, (T.lkr[0:1, :], (("lkr", None),)), True, False)
        mm(A("pcn", 0, 256, key="l"), ONE1, (T.k2b[0:1, :], (("k2b", None),)), False, False)
        mm(A("pcn", 0, 256, key="l"), ONE1, (T.cr[0:1, 768:1024], (("cr", 3),)), False, False)
        for h in range(2):
            mm(A("pcn", 128 * h, 128 * h + 128, key="l"), LFh[h], I32, False, h == 1)

        def sums_l(h):
            for dst, src, wk in (("pk", "ab", 1), ("pg", "sg", 2)):
                for k in range(16):
                    mm(A(dst, 128 * h + k, 128 * h + 128, 16),
                       (T[src][:, 2048 * h + k:2048 * h + 2048:16], ((src, 2 * h), (src, 2 * h + 1))),
                       A("gw", 8 * wk, 8 * wk + 8, key=wk), False, h == 1 and k == 15)

        def sums_c(h):
            for k in range(16):
                mm(A("pb", 128 * h + k, 128 * h + 128, 16),
                   (T.cb[:, 2048 * h + k:2048 * h + 2048:16], (("cb", 2 * h), ("cb", 2 * h + 1))),
                   A("gw", 24, 32, key=3), False, h == 1 and k == 15)

        for q in range(4):
            h, lo = q // 2, 1024 * q
            tt(A("dd", lo, lo + 1024, key=q), ind("pt", 16, 4112, "ll", c0 + 64 * q, c0 + 64 * q + 64, t),
               A("yr", lo, lo + 1024, key=h), Op.subtract)
            act(A("ab", lo, lo + 1024, key=q), A("dd", lo, lo + 1024, key=q), F.Abs)
            act(A("sg", lo, lo + 1024, key=q), A("dd", lo, lo + 1024, key=q), F.Sign, bias=-0.5)
            if q == 1:
                sums_l(0)
            if q == 2:
                ts(CF, A("cl", c0, c0 + 256, key=t), -2063.0, Op.add)
                ts(EM, A("cl", c0, c0 + 256, key=t), 16.0, Op.is_lt, 256.0, Op.mult)
                mm(A("pcn", 256, 512, key="x"), A("lb", 256 * t, 256 * t + 128, key=t), ID2, True, False)
                mm(A("pcn", 256, 512, key="x"), A("lb", 256 * t + 128, 256 * t + 256, key=t), ID2, False, False)
                mm(A("pcn", 256, 512, key="x"), H256, (T.r16[0:1, :], (("r16", None),)), False, False)
                for h in range(2):
                    mm(A("pcn", 256 + 128 * h, 384 + 128 * h, key="x"), CFh[h], I256, False, False)
                for h in range(2):
                    mm(A("pcn", 256 + 128 * h, 384 + 128 * h, key="x"), RFh[h], IDB, False, h == 1)
                for h in range(2):
                    mm(A("pe", 128 * h, 128 * h + 128, key="xs"), RFh[h], IDB, True, False)
                    mm(A("pe", 128 * h, 128 * h + 128, key="xs"), EMh[h], IDB, False, True)
        act(A("lk"), A("pcn", 0, 256, key="l"), F.Copy)
        act(A("xk"), A("pcn", 256, 512, key="x"), F.Copy)
        op("s", lambda: g.scalar.activation(T.rho[:, :], T.pe[:, 0:256], F.Identity, bias=128.53125, scale=1.0 / 32),
           [A("rho")], [A("pe", 0, 256, key="xs")])
        for q in range(4):
            h, lo = q // 2, 1024 * q
            w = ind("pt", 0, 4112, "cl", c0 + 64 * q, c0 + 64 * q + 64, t)
            tt(A("cb", lo, lo + 1024, key=q), (w[0], w[1] + (("ptz", None),)), A("yr", lo, lo + 1024, key=h), Op.is_gt)
            if q == 1:
                sums_c(0)
                sums_l(1)
        sums_c(1)
        U = L(0)
        cp(U, A("pe", 256, 272, key="u"))
        tt(I(2), U, U, Op.mult)
        ts(I(4), U, 37.0, Op.mult, float(t), Op.add)
        ts(I(3), I(2), 5, Op.arith_shift_right)
        tt(I(5), I(3), I(4), Op.add)
        ts(NEW, I(5), 4095, Op.bitwise_and)
        ts(A("smb"), A("rho"), 137.0, Op.min, -32.0, Op.mult)
        mm((T.ph[:, :], (("ph", "l"), ("ph", "x"))), H256, (T.rk0[0:1, :], (("rk0", 0), ("rk0", 1))), True, False)
        for h in range(2):
            mm(A("ph", 128 * h, 128 * h + 128, key="l"), LFh[h], D32, False, False)
        for h in range(2):
            mm(A("ph", 256 + 128 * h, 384 + 128 * h, key="x"), CFh[h], D256, False, False)
        for h in range(2):
            mm(A("ph", 256 + 128 * h, 384 + 128 * h, key="x"), RFh[h], DB, False, h == 1)
        mm(A("pf", 0, 256), I32, LF, True, False)
        mm(A("px", 256, 512, key="s"), ONE1, (T.k2b[0:1, :], (("k2b", None),)), True, False)
        mm(A("px", 256, 512, key="s"), IDB, A("smb"), False, True)
        tt(A("kg"), A("pg", 0, 256), A("lk"), Op.max)
        tt(A("qq"), A("pk", 0, 256), A("kg"), Op.min)
        tt(A("pk", 256, 512, key="b"), A("pb", 0, 256), A("xk"), Op.max)
        tt(A("key"), A("pk", 256, 512, key="b"), A("qq"), Op.min)
        scan(A("pm"), A("rs"), A("key"), 1.0e9, Op.max, Op.min)
        M = I(7)
        cp(M, A("pm", 15, 256, 16))
        a, j = I(8), I(9)
        NB32 = L(3)
        ts(a, M, 5, Op.arith_shift_right, 4095, Op.bitwise_and)
        ts(NB32, M, 16777216.0, Op.is_ge, 32.0, Op.mult)
        ts(CL32, M, 16777216.0 + 2097152.0, Op.is_ge, 32.0, Op.mult)
        ts(B32, M, 16777216.0, Op.is_lt, 32.0, Op.mult)
        tt(I(10), U, a, Op.mult)
        ts(I(11), a, float(97 * t), Op.add)
        tt(G32, NB32, CL32, Op.subtract)
        ts(I(12), I(10), 5, Op.arith_shift_right)
        ts(I(14), M, 5, Op.arith_shift_right, 7, Op.bitwise_and)
        ts(I(15), M, 1, Op.bitwise_and)
        tt(I(13), I(12), I(11), Op.add)
        ts(I(16), M, 19, Op.arith_shift_right, 2, Op.bitwise_and)
        ts(I(19), M, 30, Op.bitwise_and)
        ts(j, I(13), 3840, Op.bitwise_and)
        tt(L(5), I(15), I(16), Op.add)
        ts(CON, M, 8, Op.arith_shift_right, 4095, Op.bitwise_and)
        tt(NAM, j, A("cc"), Op.add)
        s3 = L(5)
        if t:
            tt(L(6), L(5), A("w8"), Op.add)
            s3 = L(6)
        tt(A("p3"), (T.ia[:, :], CON[1] + NEW[1] + NAM[1]), (T.fl[:, :], B32[1] + CL32[1] + G32[1]), Op.mult)
        tt(L(7), I(14), s3, Op.is_lt)
        tt(L(11), P3[0], P3[1], Op.add)
        tt(L(12), L(7), B32, Op.mult)
        tt(L(13), L(11), P3[2], Op.add)
        tt(A("srl", 0, 256, 16), L(12), I(19), Op.add)
        DL = A("ph", 0, 256, 16, key="l")
        tt(DL, DL, L(13), Op.add)
        scan(A("ra"), A("rzb"), A("srl"), 0.0, Op.mult, Op.add)
        scan(A("pk", 0, 256), A("rzf"), A("ph", 0, 256, key="l"), 0.0, Op.mult, Op.add)
        ts(A("ma"), A("ra"), 0.0, Op.is_equal)
        tt(L(23), a, G32, Op.mult)
        tt(A("dml"), A("pk", 0, 256), A("ma"), Op.mult)
        for h in range(2):
            mm(A("pf", 128 * h, 128 * h + 128), A("dml", 128 * h, 128 * h + 128), ID, False, h == 1)
        ts(L(28), j, -4096.0, Op.add, 1.0 / 8192, Op.mult)
        tt(L(29), L(23), G32, Op.add)
        tt(L(30), L(28), G32, Op.mult)
        ts(I(20), M, 21, Op.arith_shift_right)
        tt(A("zz"), L(30), L(29), Op.add)
        for i in range(16):
            act(A("zx", 16 * i, 16 * i + 16), A("mk"), F.Copy, scale=(T.zz[:, i:i + 1], (("zz", None),)))
        for h in range(2):
            mm(A("pe", 272 + 8 * h, 280 + 8 * h, key="z"), A("zx", 128 * h, 128 * h + 128), A("gsf"), True, True)
        if not last:
            for h in range(2):
                op("s", lambda: g.scalar.activation(T.wj[:, 8 * h:8 * h + 8], T.fl[:, 8 * h:8 * h + 8], F.Copy,
                                                    accum_out=T.ws[:, h:h + 1]),
                   [A("wj", key=h), A("ws", key=h)], [B32])
        scan(A("sm"), A("rs"), A("px", 256, 512, key="s"), 1.0e9, Op.max, Op.min)
        mm(A("px", 0, 256), I256, CF, True, False)
        mm(A("px", 0, 256), IDB, RF, False, False)
        ts(I(23), M, 0xFFFE0, Op.bitwise_and)
        ts(L(14), I(20), 2.0, Op.mult, 16.0, Op.add)
        cp(I(0), A("sm", 15, 256, 16))
        ts(L(15), M, 16777216.0, Op.is_lt)
        ts(L(20), I(23), 1.0 / 32, Op.mult, 1.0, Op.add)
        ts(I(1), I(0), 30, Op.bitwise_and)
        tt(L(22), B32, L(12), Op.subtract)
        tt(L(21), L(20), L(12), Op.mult)
        tt(L(16), L(14), I(1), Op.subtract)
        tt(L(24), L(23), L(22), Op.subtract)
        tt(L(26), L(21), I(19), Op.add)
        tt(L(17), L(16), L(15), Op.mult)
        ts(L(25), L(24), 8.0, Op.mult)
        if not last:
            ts(A("llo", c0, c0 + 256, key=t), A("pf", 0, 256), 1.0 / 32, Op.mult, 2048.0, Op.add)
            send("llo", "ll", "al", t)
        tt(L(18), L(17), I(1), Op.add)
        tt(L(27), L(25), L(26), Op.add)
        tt(A("srx", 0, 256, 16), L(18), CL32, Op.add)
        ts(I(24), A("pe", 272, 288, key="z"), 16.0, Op.add)
        ts(I(25), I(24), 5, Op.arith_shift_right)
        ts(I(26), I(24), 31, Op.bitwise_and)
        ts(A("aof"), I(25), 15.0, Op.add)
        ts(I(27), I(26), 256.0, Op.mult)
        w = ind("pt", 0, 4112, "aof", 0, 16, None)
        w = (w[0], w[1] + (("ptz", None),))
        Y = A("ys", 256 * par, 256 * par + 256, key=par)
        tt(A("ee"), w, Y, Op.subtract)
        act(A("ys", 256 - 256 * par, 512 - 256 * par, key=1 - par), A("ee"), F.Abs)
        if not last:
            spread(0, 1 - par)
        DX = A("ph", 256, 512, 16, key="x")
        tt(DX, DX, L(27), Op.add)
        scan(A("rb"), A("rzb"), A("srx"), 0.0, Op.mult, Op.add)
        scan(A("pk", 0, 256), A("rzf"), A("ph", 256, 512, key="x"), 0.0, Op.mult, Op.add)
        ts(A("mb"), A("rb"), 0.0, Op.is_equal)
        tt(I(28), I(27), A("cgp"), Op.add)
        tt(A("dmx"), A("pk", 0, 256), A("mb"), Op.mult)
        for h in range(2):
            mm(A("px", 128 * h, 128 * h + 128), A("dmx", 128 * h, 128 * h + 128), ID, False, h == 1)
        ts(A("mn"), A("ee"), 0.0, Op.min)
        cp(A("nof"), I(28))
        op("v", lambda: g.vector.tensor_tensor(T.pt[:, 16:PW].indirect(T.nof[:, 0:16]), A("mn")[0], Y[0], Op.add),
           [A("pt")], [A("mn"), Y, A("nof")])
        if not last:
            ts(A("clo", c0, c0 + 256, key=t), A("px", 0, 256), 1.0 / 256, Op.mult, 2062.502, Op.add)
            send("clo", "cl", "ac", t)
            act(A("xn"), A("px", 0, 256), F.Copy)
            spread(1, 1 - par)
            ts(A("wi", 0, 2), (T.ws[:, 0:2], (("ws", 0), ("ws", 1))), 1.0 / 32, Op.mult)
            ts(A("wk", 0, 2), A("wi", 0, 2), 3, Op.bitwise_and)
            cp(A("wf", 0, 2), A("wk", 0, 2))
            CN = A("cf", 256 - 256 * par, 512 - 256 * par, key=1 - par)
            ts(CN, A("clo", c0, c0 + 256, key=t), -2063.0, Op.add)
            mm(A("pf", 256, 512, key="r"), ID, A("xn"), True, False)
            mm(A("pf", 256, 512, key="r"), IM256, CN, False, True)
            act(A("rlo", c0, c0 + 256, key=t), A("pf", 256, 512, key="r"), F.Copy)
            send("rlo", "rl", "ar", t)
            for h in range(2):
                op("s", lambda: g.scalar.activation(T.w8[:, 8 * h:8 * h + 8], T.onf[:, 0:8], F.Copy, scale=T.wf[:, h:h + 1]),
                   [A("w8")], [A("onf"), A("wf", 0, 2)], selfok=True)

    dma("y", T.zp[:, :], T.pt[:, 16:4112], "o0", [("zp", None)], [("pt", None)])
    dma("s", T.zy[:, :], T.ys[:, 0:256], "o1", [("zy", None)], [("ys", 0)])
    ts(A("ofl"), A("pf", 0, 256), 1.0 / 32, Op.mult, 2048.0, Op.add)
    dma("y", T.zl[:, :], T.ofl[:, :], "o2", [("zl", None)], [("ofl", None)])
    ts(A("xsi"), A("px", 0, 256), 524032.0, Op.add)
    ts(A("oi", 0, 256, key=0), A("xsi"), 8, Op.arith_shift_right)
    ts(A("oi", 256, 512, key=1), A("xsi"), 1, Op.arith_shift_right, 15, Op.bitwise_and)
    ts(A("oi", 512, 768, key=2), A("xsi"), 5, Op.arith_shift_right, 7, Op.bitwise_and)
    cp(A("ofc"), A("oi", 0, 256, key=0))
    dma("y", T.zc[:, :], T.ofc[:, :], "o3", [("zc", None)], [("ofc", None)])
    cp(A("obo"), A("oi", 256, 512, key=1))
    dma("s", T.zo[:, :], T.obo[:, :], "o4", [("zo", None)], [("obo", None)])
    cp(A("obb"), A("oi", 512, 768, key=2))
    dma("y", T.zb[:, :], T.obb[:, :], "o5", [("zb", None)], [("obb", None)])
    for q in ("v", "s", "t", "p"):
        if known["p"].get(own[q], 0) < count[q]:
            g.wait_ge(T.sem[own[q]], count[q])
    g.wait_ge(T.sem.loc, sent[0])
    for i in range(6):
        g.wait_ge(T.sem["o%d" % i], 16)
